import numpy as np, ml_dtypes
CORES = [23,119,17,113]
N = 4
import mx_ref
BF = ml_dtypes.bfloat16
def gcols(t, e):
    v = np.concatenate([t.reshape(8, 16, -1, 4), np.zeros((8, 16, 1, 4), BF)], axis=2)
    return np.ascontiguousarray(np.stack([v[g][:, e[g]] for g in range(8)])).reshape(128, -1)
def tile(rs):
    return np.stack(rs, axis=2).reshape(128, -1).astype(BF)
def pick(q, e):
    c = np.concatenate([q[0].reshape(128, -1, 4), np.zeros((128, 1, 4), np.uint8)], axis=1); s = np.concatenate([q[1], np.ones((16, 1), np.uint8)], axis=1)
    return (np.ascontiguousarray(c[:, e].reshape(128, -1)), np.ascontiguousarray(s[:, e]))
def join(*qs):
    return (np.concatenate([q[0] for q in qs], axis=1), np.concatenate([q[1] for q in qs], axis=1))
def put(q, e, v):
    c, s = q[0].reshape(128, -1, 4).copy(), q[1].copy(); c[:, e] = v[0].reshape(128, -1, 4); s[:, e] = v[1]
    return (c.reshape(128, -1), s)
def pk(c, s):
    return (np.ascontiguousarray(c), mx_ref.live(s))
def emit(q):
    return q[0], q[1]
def packed(v, rng):
    q = [mx_ref.quantize(np.ascontiguousarray(v[r])) for r in range(N)]
    return np.stack([a for a, b in q]), np.stack([mx_ref.plane(b, rng) for a, b in q])
def values_of_codes():
    e, c = np.zeros((128, 128, 4), np.float32), np.zeros((128, 2, 4), np.uint8)
    e[np.arange(128), np.arange(128), 0] = 1
    c[:127, :, 0] = np.arange(256).reshape(2, 128).T[:127]
    return mx_ref.matmul(mx_ref.quantize(e.reshape(128, 512).astype(BF)), (c.reshape(128, 8), np.full((16, 2), 127, np.uint8))).T.reshape(-1).astype(np.float64)
CODE_VALUE, SCALE_VALUE = values_of_codes(), 2.0 ** (np.arange(256) - 127.0)
def decode(q):
    return (CODE_VALUE[q[0]].reshape(16, 8, -1, 4) * SCALE_VALUE[q[1]][:, None, :, None] + 0.0).reshape(128, -1).astype(np.float32)
def f(rng, *shape):
    return mx_ref.flush((rng.standard_normal(shape, dtype=np.float32) * np.exp2(rng.integers(-2, 3, shape[:-1] + (1,)))).astype(BF))
def wide(rng, *shape, cols=0):
    v = rng.standard_normal(shape, dtype=np.float32) * np.exp2(rng.integers(-12, 13, shape)).astype(np.float32)
    if cols: v *= np.repeat(np.exp2(rng.integers(-cols, cols + 1, shape[:-2] + (1, shape[-1] // 4))) * (rng.random(shape[:-2] + (1, shape[-1] // 4)) > 0.0625), 4, axis=-1).astype(np.float32)
    return mx_ref.flush(v.astype(BF))
C, R = 448, 2
STEP = [1, 2]
def units(s, way):
    p = s[::16] + np.float32(0.0)
    n = 1 + (s[1::16] > 0) + (s[2::16] > 0) + (s[3::16] > 0)
    o = np.argsort(np.float32(way) * p, axis=1, kind="stable")
    return [np.repeat(o[g], n[g][o[g]]) for g in range(8)]
def segments(bids, asks):
    e, first = np.zeros((2, 8, C), np.int64), np.full((2, 8, C), -1)
    for g in range(8):
        m = min(len(bids[g]), len(asks[g]))
        a = np.stack([bids[g][:m], asks[g][:m]])
        new = np.concatenate([[True], (a[:, 1:] != a[:, :-1]).any(axis=0)])
        e[:, g] = a[:, np.flatnonzero(new)[:C]]
        for i in range(2):
            c, k = np.unique(e[i, g], return_index=True)
            first[i, g, c] = k
    return e, first
def numbers_of(rng):
    return {"x": np.array(f(rng, N, 128, 4 * C)), "u": np.stack([f(rng, 128, 512)] * N), "v": np.array(f(rng, N, 128, 512))}
def common(w, rng):
    c, p = packed(np.stack([w] * N), rng)
    return {"wc": c, "ws": p}
def planted(rng, s, n, less=()):
    d = numbers_of(rng)
    kind = rng.permutation(8) % 3
    sign = np.stack([rng.permutation(8) % 2 * 2.0 - 1.0 for r in range(N)])
    k = np.where(kind > 0, 2.0 ** -30, 1.0)
    x = d["x"].astype(np.float32).reshape(N, 8, 16, C, 4)
    e = ((s[..., None] >> np.arange(8)) & 1) * np.exp2(np.arange(8) - 23.0)
    e = e * np.where(kind == 2, sign * 2.0 ** -7, 1.0)[:, :, None, None] + 0.0
    one = np.repeat(np.where(kind < 2, sign, 0.0)[:, :, None], C, axis=2)
    for r in range(N):
        for g in rng.permutation(8)[:4]: one[r, g, rng.integers(C)] = sign[r, g] * 2.0 ** 30
    price = one + np.sum(e, axis=3)
    for r, g in less:
        n[r, g, np.argmin(price[r, g]) if r % 2 else np.argmax(price[r, g])] = 2
    q = np.where(np.argsort(rng.random((N, 8, C, 3)), axis=3) < n[..., None] - 1, 1, -rng.integers(0, 2, (N, 8, C, 3)))
    x[:, :, 0] = 0
    x[:, :, 0, :, 0] = one
    x[:, :, 8] = e[..., :4]
    x[:, :, 9] = e[..., 4:]
    x[:, :, 10] = 0
    x[:, :, 10, :, :3] = q * np.where(kind == 2, 2.0 ** -30, 2.0 ** -20)[:, None, None]
    x[:, :, 11:] = rng.integers(4, 8, (N, 8, 5, C, 4)) * rng.choice([-1.0, 1.0], (N, 8, 5, C, 4)) * 2.0 ** -20
    u = d["u"][0].astype(np.float32).reshape(128, 128, 4)
    for g in range(8):
        h = 16 * g
        u[:, h:h + 4] = 0
        u[h, h, 0] = k[g]
        u[h + 8:h + 10, h] = k[g]
        for i in range(3): u[h + 10, h + 1 + i, i] = k[g]
    w = np.array(f(rng, 128, 2048)).reshape(128, 4, 8, 16, 4)
    w[::16] = 0
    w[:, :, :, 0] = 0
    w[:, :, :, 8:] = 0
    return {"x": x.reshape(N, 128, 4 * C).astype(BF), "u": np.stack([u.reshape(128, 512).astype(BF)] * N), "v": d["v"], **common(w.reshape(128, 2048), rng)}
def pairs_of(rng):
    return np.argsort(rng.random((N, 8, C)), axis=2) // 2
def setup_inputs(rng):
    return {**numbers_of(rng), **common(f(rng, 128, 2048), rng)}
def setup_inputs_ties(rng):
    d = numbers_of(rng)
    o = rng.permutation(N)
    x = d["x"].reshape(N, 8, 16, C, 4)
    for r in range(N):
        k = np.zeros(C, int) if r == o[0] else rng.permutation(C) % 3
        a = x[r][:, :8, :3].copy()
        a[:, :, 2] = 0
        x[r][:, :8] = a[:, :, k]
    x[o[1]] = 0
    u = d["u"].reshape(N, 8, 16, 128, 4)
    u[:, :, 8:, ::16] = 0
    w = np.array(f(rng, 128, 2048)).reshape(128, 4, 8, 16, 4)
    w[:, :, :, :8] = 0
    return {"x": x.reshape(N, 128, 4 * C), "u": u.reshape(N, 128, 512), "v": d["v"], **common(w.reshape(128, 2048), rng)}
def setup_inputs_near(rng):
    return planted(rng, pairs_of(rng), rng.integers(1, 5, (N, 8, C)))
def setup_inputs_lots(rng):
    n = np.zeros((N, 8, C), np.int64)
    p = rng.permutation(N // 2)
    h = rng.permutation(8) % 2
    less = []
    for i in range(N // 2):
        c = (p[i] + N // 2 * h) % 4
        k = np.array([(1, 4), (2, 3), (4, 4), (1, 1)])[c]
        j = int(rng.integers(2))
        n[2 * i], n[2 * i + 1] = k[:, j, None], k[:, 1 - j, None]
        g = rng.permutation(np.flatnonzero(c == 2))
        less += [(2 * i, int(a)) for a in g[::4]] + [(2 * i + 1, int(a)) for a in g[1::4]]
    return planted(rng, pairs_of(rng), n, less)
def setup_inputs_huge(rng):
    d = numbers_of(rng)
    x = 2.0 ** 30 * (0.6 + 0.2 * rng.random((N, 128, C, 4)))
    c = np.stack([rng.permutation(C) % 2 * 2.0 - 1.0 for r in range(N)])
    o = rng.permutation(N)
    c[o < N // 2] = 1
    c[o == 0] = -1
    x *= c[:, None, :, None]
    u = d["u"][0].astype(np.float32).reshape(128, 128, 4)
    u[:, ::16] = 2.0 ** 30 * (1 - 0.25 * rng.random((128, 8, 4))) * (rng.permutation(8) % 2 * 2.0 - 1.0)[None, :, None]
    w = np.zeros((128, 4, 128, 4), np.float32)
    i = np.arange(128)
    for b in range(4): w[i, b, i, b] = 1
    return {"x": x.astype(np.float32).reshape(N, 128, 4 * C).astype(BF), "u": np.stack([u.reshape(128, 512).astype(BF)] * N), "v": d["v"], **common(w.reshape(128, 2048).astype(BF), rng)}
def setup_inputs_spread(rng):
    d = setup_inputs(rng)
    d["x"] = wide(rng, N, 128, 4 * C, cols=6)
    return d
def check_inputs(d):
    b = []
    for k in ("x", "u", "v"):
        a = np.abs(d[k].astype(np.float32))
        if not (np.isfinite(a).all() and ((a == 0) | (a >= 2.0 ** -30) & (a <= 2.0 ** 30)).all()): b.append("a value of " + k)
    a = d["u"].astype(np.float32)
    if (a != a[:1]).any(): b.append("u differs between ranks")
    if (d["wc"] != d["wc"][:1]).any(): b.append("wc differs between ranks")
    s = [mx_ref.live(p) for p in d["ws"]]
    if any((p != s[0]).any() for p in s): b.append("ws differs between ranks")
    return b
def reference(x, u, v, wc, ws):
    w = pk(wc[0], ws[0])
    lay = [pick(w, np.arange(128 * b, 128 * b + 128)) for b in range(4)]
    qu = mx_ref.quantize(u[0])
    now = [x[r] for r in range(N)]
    lists = [None] * N
    for t in range(R):
        held, score = [], []
        for r in range(N):
            q = mx_ref.quantize(now[r])
            held.append(decode(q).astype(BF))
            score.append(mx_ref.matmul(qu, q))
        for r in range(N):
            s = r ^ STEP[t]
            if s < r: continue
            e, first = segments(units(score[r], -1), units(score[s], 1))
            z = gcols(held[r], e[0]).astype(np.float32) + gcols(held[s], e[1]).astype(np.float32)
            q = mx_ref.quantize((z * np.float32(0.5)).astype(BF))
            h = tile([np.maximum(mx_ref.matmul(lay[b], q), np.float32(0.0)) * np.float32(0.03125) for b in range(4)])
            h = decode(mx_ref.quantize(h)).astype(BF)
            for i, k in ((0, r), (1, s)):
                now[k] = (held[k].astype(np.float32) + gcols(h, first[i]).astype(np.float32)).astype(BF)
                lists[k] = first[i]
    y, ol = np.zeros((N, 128, C), np.float32), np.zeros((N, 8, C), np.float32)
    oc, osc = np.zeros((N, 128, 4 * C), np.uint8), np.zeros((N, 16, C), np.uint8)
    for r in range(N):
        q = mx_ref.quantize(now[r])
        y[r] = mx_ref.matmul(mx_ref.quantize(v[r]), q)
        ol[r] = lists[r]
        oc[r], osc[r] = emit(q)
    return {"y": y, "ol": ol, "oc": oc, "osc": osc}

@@ -1,0 +1,440 @@
+from concourse.mybir import dt, AluOpType, ActivationFunctionType
+
+C = 448
+K = C // 16
+NB = C // 32
+UN = 4 * C
+HW = C + 16
+H, KH = C // 2, K // 2
+BIG = float(2 ** 19)
+LOW = -(2 ** 20)
+STEP = [1, 2]
+SWAP_LISTS = [True, True]
+SPLIT_LISTS = True
+SCALAR_LEFT = []
+NSG, NG = 5, 3
+
+F32, BF, I32, U16, CODE, U8 = "float32", "bfloat16", "int32", "uint16", "float8_e4m3fn_x4", "uint8"
+SCRATCH = {}
+for _n, _w, _d in [
+        ("X0", 4 * C, BF), ("X1", 4 * C, BF), ("X2", 4 * C, BF), ("UB", 512, BF), ("VB", 512, BF),
+        ("UQ", 128, CODE), ("US", 128, U8), ("UP", 256, CODE), ("UPS", 256, U8), ("VQ", 128, CODE), ("VS", 128, U8),
+        ("WQ", 512, CODE), ("WS", 512, U8), ("EB", 2048, BF), ("EQ", 512, CODE), ("ES", 512, U8),
+        ("CB", 512, BF), ("CQ", 128, CODE), ("CS", 128, U8),
+        ("I1", 128, F32), ("I2", 128, F32), ("I3", 64, F32), ("PI", 2, I32), ("PJ", 4, I32), ("PF", 4, F32),
+        ("UI", 16, I32), ("UO", 16, U16), ("K16", 16, F32), ("XA", 16, F32), ("XB", 16, F32), ("XC", 16, F32),
+        ("RO", K, U16), ("XP", C, F32), ("XO", 4, F32), ("TR", 64, BF), ("QP", 3 * K, F32), ("IO", HW, F32),
+        ("ONE", C, BF), ("M512", C, F32),
+        ("TQ0", C, CODE), ("TS0", C, U8), ("TQ1", C, CODE), ("TS1", C, U8), ("TQ2", C, CODE), ("TS2", C, U8),
+        ("LQ0", C, CODE), ("LS0", C, U8), ("LQ1", C, CODE), ("LS1", C, U8),
+        ("ST", C, F32), ("QF", 3 * K, F32), ("Q3", 3 * K, F32), ("QN", 3 * K, F32),
+        ("EX", C, F32), ("EY", C, F32), ("FR", C, F32), ("FP", C, F32), ("FI", C, F32), ("FJ", C, F32),
+        ("SO0", K, U16), ("SO1", K, U16), ("SP0", K, U16), ("SP1", K, U16),
+        ("LO0", 32, U16), ("LO1", 32, U16), ("LP0", 32, U16), ("LP1", 32, U16),
+        ("FO", K, U16), ("FS", K, U16), ("FT", K, U16), ("LI", K, I32), ("LJ", K, I32), ("LK", K, I32), ("LL", K, I32),
+        ("FW", K, F32), ("FV", K, F32), ("NO", K, I32), ("HO", K, I32), ("EO", K, I32), ("GO", K, U16),
+        ("NP", K, I32), ("HPI", K, I32), ("EP", K, I32), ("GP", K, U16),
+        ("MK0", UN, BF), ("MK1", UN, BF), ("SEG", UN // 2 + 16, F32),
+        ("AO0", 2 * C, F32), ("AO1", 2 * C, F32), ("AP0", 2 * C, F32), ("AP1", 2 * C, F32),
+        ("DO", 4 * C, BF), ("DP", 4 * C, BF), ("ZT", 4 * C, BF), ("Z", 4 * C, BF), ("ZQ", C, CODE), ("ZS", C, U8),
+        ("HP", 4 * HW, BF), ("HT", 4 * C, BF), ("HQ", C, CODE), ("HS", C, U8), ("YS", C, F32), ("OL", C, F32)]:
+    SCRATCH[_n] = ("sbuf", [128, _w], _d)
+for _i in range(NSG):
+    SCRATCH["SG%d" % _i] = ("sbuf", [128, 2 * C], BF)
+for _i in range(NG):
+    SCRATCH["G%d" % _i] = ("sbuf", [128, 4 * C], BF)
+    SCRATCH["GQ%d" % _i] = ("sbuf", [128, C], CODE)
+    SCRATCH["GS%d" % _i] = ("sbuf", [128, C], U8)
+for _i in range(8):
+    SCRATCH["ps%d" % _i] = ("psum", [128, 512], F32)
+SEMAPHORES = ["cv", "cs", "ct", "cg", "dx0", "dx1", "du", "dv", "dw", "dol", "sent",
+              "rT0", "rT1", "rS0", "rS1", "rL00", "rL01", "rL10", "rL11", "dst"]
+
+A = AluOpType
+AF = ActivationFunctionType
+
+
+def rank_program(g, core, T, topo):
+    rank = T.rank_of(core)
+    if rank is None:
+        return
+    q = {"v": g.vector, "s": g.scalar, "t": g.tensor, "g": g, "y": g.sync}
+    own = {"v": "cv", "s": "cs", "t": "ct", "g": "cg"}
+    total = {n: 0 for n in SEMAPHORES}
+    waited = {n: 0 for n in SEMAPHORES}
+    clock = {e: {} for e in q}
+    snap, writer, readers = {}, {}, {}
+
+    def need(e, tok):
+        s, n = tok
+        if clock[e].get(s, 0) >= n:
+            return
+        q[e].wait_ge(T.sem[s], n)
+        waited[s] = max(waited[s], n)
+        for k, m in list(snap.get(tok, {}).items()) + [(s, n)]:
+            clock[e][k] = max(clock[e].get(k, 0), m)
+
+    def order(e, rd, wr, acc):
+        toks = []
+        for k in rd:
+            toks += writer.get(k, [])
+            if k.startswith("ps"):
+                toks += [t for f, t in readers.get(k, []) if f != e]
+        for k in wr:
+            if not acc:
+                toks += writer.get(k, [])
+            toks += [t for f, t in readers.get(k, [])]
+        best = {}
+        for s, n in toks:
+            best[s] = max(best.get(s, 0), n)
+        for s in sorted(best, key=lambda s: -len(snap.get((s, best[s]), {}))):
+            need(e, (s, best[s]))
+
+    def done(e, tok, rd, wr):
+        snap[tok] = dict(clock[e])
+        for k in rd:
+            readers.setdefault(k, []).append((e, tok))
+        for k in wr:
+            writer[k] = [tok]
+            readers[k] = []
+
+    def op(e, call, rd, wr, acc=False):
+        order(e, rd, wr, acc)
+        s = own[e]
+        call(q[e]).then_inc(T.sem[s], 1)
+        total[s] += 1
+        done(e, (s, total[s]), rd, wr)
+
+    def dma(e, sem, items):
+        tok = (sem, total[sem] + 16 * len(items))
+        for out, in_, rd, wr in items:
+            order(e, rd, wr, False)
+            q[e].dma_start(out, in_).then_inc(T.sem[sem], 16)
+        total[sem] = tok[1]
+        for out, in_, rd, wr in items:
+            done(e, tok, rd, wr)
+
+    def send(dst, sem, items):
+        rid, pid, se = topo.addr(dst)
+        m = topo.mask(core, dst)
+        n = len(topo.engines(core, dst))
+        for out, in_, rd, land in items:
+            order("g", rd, [], False)
+            g.remote_dma(out, in_, T.sem[sem], T.sem["sent"], pid, rid, m)
+            total["sent"] += n
+            total[sem] += len(topo.engines(dst, core))
+        for out, in_, rd, land in items:
+            for k in land:
+                writer[k] = [(sem, total[sem])]
+
+    def ts(e, out, in0, s1, s2, o0, o1, rd, wr):
+        if s2 is None:
+            op(e, lambda E: E.tensor_scalar(out, in0, s1, None, o0), rd, wr)
+        else:
+            op(e, lambda E: E.tensor_scalar(out, in0, s1, s2, o0, o1), rd, wr)
+
+    def tt(out, a, b, o, rd, wr):
+        op("v", lambda E: E.tensor_tensor(out, a, b, o), rd, wr)
+
+    def cp(e, out, in_, rd, wr, scale=None):
+        if e == "v":
+            op(e, lambda E: E.tensor_copy(out, in_), rd, wr)
+        elif scale is None:
+            op(e, lambda E: E.activation(out, in_, AF.Copy), rd, wr)
+        else:
+            op(e, lambda E: E.activation(out, in_, AF.Copy, scale=scale), rd, wr)
+
+    def fill(out, val, wr):
+        op("v", lambda E: E.memset(out, val), [], wr)
+
+    def iota(name, out, pat, base, cm, ints=False):
+        if ints:
+            op("g", lambda E: E.iota(out, pat, base, cm), [], [name])
+        else:
+            op("g", lambda E: E.iota(out, pat, base, cm, allow_small_or_imprecise_dtypes=True), [], [name])
+
+    def quant(qn, sn, a, b, tile, rd):
+        op("v", lambda E: E.quantize_mx(T[qn][:, a:b], T[sn][:, a:b], T[tile][:, 4 * a:4 * b]), rd, [qn + "_%d" % a])
+
+    def mm(bank, wq, ws, wa, xq, xs, start, stop, rd, a=0, b=C):
+        bank = "ps%d" % bank
+        op("t", lambda E: E.matmul_mx(T[bank][:, 0:b - a], T[wq][:, wa:wa + 128], T[ws][:, wa:wa + 128],
+                                      T[xq][:, a:b], T[xs][:, a:b], start, stop), rd, [bank], acc=not start)
+
+    def scan(out, d0, d1, init, o0, o1, rd, wr):
+        op("v", lambda E: E.tensor_tensor_scan(out, d0, d1, init, o0, o1), rd, wr)
+
+    def wrap(dst, src, rd, wr, a=0, b=C):
+        scan(T[dst][:, a:b], T[src][:, a:b], T.XP[:, a:b], float(LOW), A.max, A.add, rd + ["XP"], wr)
+
+    def slots(n, k=""):
+        return [n + "_%d%s" % (b, k) for b in range(4)]
+
+    def both(n):
+        return [n + "_0", n + "_%d" % H]
+
+    def halves(n):
+        return [n + "h0", n + "h1"]
+
+    def scores(t, k):
+        mm(4 + k, "UQ", "US", 0, "TQ%d" % t, "TS%d" % t, True, True, ["UQ_0", "TQ%d_%d" % (t, H * k)], H * k, H * k + H)
+
+    def turn(k, negate):
+        a, c, w = H * k, 3 * KH * k, 3 * KH
+        op("v", lambda E: E.transpose(T.ST[:, a:a + H], T["ps%d" % (4 + k)][:, 0:H]), ["ps%d" % (4 + k)], ["ST%d" % k])
+        for i in range(3):
+            ts("v", T.QF[:, c + i:c + w:3], T.ST[:, a + 1 + i:a + H:16], 0.0, None, A.is_gt, None,
+               ["ST%d" % k], ["QF_%d%d" % (i, k)])
+        scan(T.Q3[:, c:c + w], T.QP[:, 0:w], T.QF[:, c:c + w], 1.0, A.min, A.add,
+             ["QP"] + ["QF_%d%d" % (i, k) for i in range(3)], ["Q3%d" % k])
+        if negate and any(2 * b // NB == k for b in SCALAR_LEFT):
+            ts("v", T.QN[:, c:c + w], T.Q3[:, c:c + w], -1.0, None, A.mult, None, ["Q3%d" % k], ["QN%d" % k])
+
+    dma("s", "du", [(T.UB[:], T.u[:], [], ["UB"])])
+    for k in range(2):
+        dma("y", "dx%d" % k, [(T.X0[:, 4 * H * k:4 * H * k + 4 * H], T.x[:, 4 * H * k:4 * H * k + 4 * H], [], slots("X0", k))])
+    need("y", ("dx1", 16))
+    dma("y", "dw", [(T.WQ[:].bitcast(dt.uint8), T.wc[:], [], ["WQ"]), (T.WS[:], T.ws[:], [], ["WS"])])
+    dma("y", "dv", [(T.VB[:], T.v[:], [], ["VB"])])
+    iota("UI", T.UI[:], [[16, 2], [32, 4], [0, 2]], 0, 0, True)
+    iota("PI", T.PI[:], [[15, 2]], 0, 1, True)
+    iota("K16", T.K16[:], [[1, 16]], 0, 0)
+    iota("I2", T.I2[:], [[1, 8], [0, 16]], 0, 0)
+    iota("I3", T.I3[:], [[1, 32], [0, 2]], 0, 0)
+    iota("I1", T.I1[:], [[1, 128]], 0, -1)
+    fill(T.QP[:], 1000.0, ["QP"])
+    fill(T.SEG[:, 0:16], 0.0, ["SEG"])
+    fill(T.ONE[:], 1.0, ["ONE"])
+    fill(T.QP[:, 0:3 * K:3], 1.0, ["QP"])
+    cp("v", T.UO[:], T.UI[:], ["UI"], ["UO"])
+    ts("v", T.PJ[:, 0:2], T.PI[:], 15, None, A.bitwise_and, None, ["PI"], ["PJ0"])
+    ts("v", T.PJ[:, 2:3], T.PI[:, 0:1], 31, None, A.bitwise_and, None, ["PI"], ["PJ2"])
+    ts("v", T.PJ[:, 3:4], T.PI[:, 0:1], 5, None, A.logical_shift_right, None, ["PI"], ["PJ3"])
+    cp("v", T.PF[:], T.PJ[:], ["PJ0", "PJ2", "PJ3"], ["PF"])
+    ts("v", T.XO[:, 3:4], T.PF[:, 3:4], 2.0, None, A.mult, None, ["PF"], ["XO3"])
+    ts("v", T.XA[:], T.K16[:], T.PF[:, 0:1], BIG, A.is_equal, A.mult, ["K16", "PF"], ["XA"])
+    ts("v", T.XB[:], T.K16[:], T.PF[:, 1:2], -2 * BIG, A.is_equal, A.mult, ["K16", "PF"], ["XB"])
+    ts("v", T.RO[:], T.I2[:, 0:K], 0.0, T.PF[:, 0:1], A.mult, A.add, ["I2", "PF"], ["RO"])
+    for k, off in ((0, -BIG), (1, -BIG - 1.0), (2, -BIG + 2.0 ** 18)):
+        ts("v", T.XO[:, k:k + 1], T.XA[:, 0:1], 2.0, off, A.mult, A.add, ["XA"], ["XO%d" % k])
+    tt(T.XC[:], T.XA[:], T.XB[:], A.add, ["XA", "XB"], ["XC"])
+    ts("v", T.TR[:], T.I3[:], T.PF[:, 2:3], 0.5, A.is_gt, A.mult, ["I3", "PF"], ["TR"])
+    for t in range(4):
+        ts("v", T.CB[:, t:512:4], T.I2[:], T.XO[:, 3:4], float(t % 2), A.subtract, A.is_equal, ["I2", "XO3"], ["CB_%d" % t])
+    quant("UQ", "US", 0, 128, "UB", ["UB"])
+    cp("s", T.UPS[:], T.US[:].indirect(T.UO[:]), ["UQ_0", "UO"], ["UPS"])
+    cp("s", T.XP[:], T.XC[:].indirect(T.RO[:]), ["XC", "RO"], ["XP"])
+    cp("v", T.UP[:].bitcast(dt.uint32), T.UQ[:].bitcast(dt.uint32).indirect(T.UO[:]), ["UQ_0", "UO"], ["UP"])
+    quant("TQ0", "TS0", 0, H, "X0", slots("X0", 0))
+    scores(0, 0)
+    quant("CQ", "CS", 0, 128, "CB", slots("CB"))
+    quant("TQ0", "TS0", H, C, "X0", slots("X0", 1))
+
+    for t in range(2):
+        mate = rank ^ STEP[t]
+        dst = T.cores[mate]
+        buys = rank < mate
+        swap = SWAP_LISTS[t]
+        n = str(t)
+        XN, NQ, NS = "X" + str(t + 1), "TQ" + str(t + 1), "TS" + str(t + 1)
+        TQ, TS, LQ, LS = "TQ" + n, "TS" + n, "LQ" + n, "LS" + n
+        SO, SP, LO, LP, MK, AO, AP = "SO" + n, "SP" + n, "LO" + n, "LP" + n, "MK" + n, "AO" + n, "AP" + n
+        for h in range(2):
+            mm(h, "UP", "UPS", 128 * h, TQ, TS, True, True, ["UP", "UPS"] + both(TQ))
+        scores(t, 1)
+        send(dst, "rT" + n, [(T[LQ][:].bitcast(dt.uint8), T[TQ][:].bitcast(dt.uint8), both(TQ), [LQ]),
+                             (T[LS][:], T[TS][:], both(TQ), [LS])])
+        iota(MK, T[MK][:], [[0, UN]], 0, 0)
+        if t == 0:
+            iota("EB_0", T.EB[:], [[0, 2048]], 0, 0)
+            for b in range(1, 4):
+                writer["EB_%d" % b] = writer["EB_0"]
+            iota("IO", T.IO[:, 0:C], [[1, C]], 0, 0)
+            iota("M512", T.M512[:], [[0, C]], -512, 0)
+        iota(AO, T[AO][:, 0:C], [[0, C]], LOW, 0)
+        if not swap:
+            iota(AP, T[AP][:, 0:C], [[0, C]], LOW, 0)
+        if t == 0:
+            for b in range(4):
+                iota("HPz%d" % b, T.HP[:, HW * b + C:HW * b + HW], [[0, HW - C]], 0, 0)
+            iota("IOz", T.IO[:, C:HW], [[0, HW - C]], -1, 0)
+        turn(0, not buys)
+        strict, loose = (A.is_gt, A.is_ge) if buys else (A.is_lt, A.is_le)
+
+        def pack(i):
+            j = str(i % NG)
+            quant("GQ" + j, "GS" + j, 0, C, "G" + j, slots("G" + j, "l") + slots("G" + j, "r"))
+            mm(3, "CQ", "CS", 0, "GQ" + j, "GS" + j, i == 0, i == NB // 2 - 1, ["CQ_0", "GQ" + j + "_0"])
+
+        def signs(b):
+            sg = "SG%d" % (b % NSG)
+            for h in range(2):
+                c = 32 * b + 16 * h
+                op("s", lambda E: E.activation(T[sg][:, h:2 * C:2], T["ps%d" % h][:, 0:C], AF.Sign,
+                                               bias=T.ST[:, c:c + 1], scale=-1.0),
+                   ["ps%d" % h, "ST%d" % (2 * b // NB)], [sg + "_%d" % h] + [sg + "d"] * (1 - h))
+
+        signs(0)
+        for b in range(NB):
+            sg, half = "SG%d" % (b % NSG), str(2 * b // NB)
+            if b + 1 < NB:
+                signs(b + 1)
+            d = T[sg][:, 64 * b:64 * b + 64]
+            tt(d, d, T.TR[:], A.add if buys else A.subtract, [sg + "_0", sg + "_1", "TR"], [sg + "d"])
+            if b % 2 == 0 and b > 0:
+                pack(b // 2 - 1)
+            gn, e = "G%d" % (b // 2 % NG), 32 * b + 32
+            for side in "rl":
+                for h in range(2):
+                    k, c = 2 * (b % 2) + h, 3 * (2 * b + h) + 2
+                    w = T.Q3[:, c:c + 1]
+                    eng = "s" if side == "l" and b in SCALAR_LEFT else "v"
+                    part = [gn + "_%d%s" % (k, side)]
+                    if side == "r" and e < C:
+                        ts("v", T[gn][:, 4 * e + k:4 * C:4], T[sg][:, 2 * e + h:2 * C:2], 0.0, w, loose, A.mult,
+                           [sg + "_%d" % h, "Q3" + half], part)
+                    elif side == "l" and eng == "v":
+                        ts("v", T[gn][:, k:4 * e:4], T[sg][:, h:2 * e:2], 0.0, w, strict, A.mult,
+                           [sg + "_%d" % h, sg + "d", "Q3" + half], part)
+                    elif side == "l":
+                        wn = "Q3" if buys else "QN"
+                        op("s", lambda E: E.activation(T[gn][:, k:4 * e:4], T[sg][:, h:2 * e:2], AF.Relu,
+                                                       scale=T[wn][:, c:c + 1]), [sg + "_%d" % h, sg + "d", wn + half], part)
+            if b == 0:
+                turn(1, not buys)
+                if t > 0:
+                    for c in range(4):
+                        mm(4 + c, "EQ", "ES", 128 * c, TQ, TS, True, True, ["EQ_0"] + both(TQ))
+        pack(NB // 2 - 1)
+        if t == 0:
+            for b in range(4):
+                ts("v", T.EB[:, 512 * b + b:512 * b + 512:4], T.I1[:], 0.0, None, A.is_equal, None, ["I1"], ["EB_%d" % b])
+        wrap("EX", "ps3", ["ps3"], halves("EX"))
+        ts("v", T[SO][:], T.EX[:, 15:C:16], T.XO[:, 0:1], None, A.add, None, halves("EX") + ["XO0"], [SO])
+        send(dst, "rS" + n, [(T[SP][:], T[SO][:], [SO], [SP])])
+        ts("v", T.NO[:], T.EX[:, 15:C:16], T.XO[:, 0:1], 1.0, A.add, A.add, halves("EX") + ["XO0"], ["NO"])
+        if t == 0:
+            quant("EQ", "ES", 0, 512, "EB", slots("EB"))
+            for b in range(4):
+                mm(4 + b, "EQ", "ES", 128 * b, TQ, TS, True, True, ["EQ_0"] + both(TQ))
+
+        def pair_of(nxt, half, even):
+            ts("v", T[half][:], T[nxt][:], 1, None, A.logical_shift_right, None, [nxt], [half])
+            ts("v", T[even][:], T[nxt][:], 1, None, A.bitwise_and, None, [nxt], [even])
+
+        cp("v", T[MK][:].indirect(T[SO][:]), T.ONE[:], [SO, "ONE"], [MK])
+        pair_of("NO", "HO", "EO")
+        if t == 1:
+            quant("VQ", "VS", 0, 128, "VB", ["VB"])
+        cp("v", T.GO[:], T.HO[:], ["HO"], ["GO"])
+        for b in range(4):
+            cp("s", T.DO[:, C * b:C * b + C], T["ps%d" % (4 + b)][:, 0:C], ["ps%d" % (4 + b)], ["DO_%d" % b], 0.5)
+        for b in range(4):
+            mm(b, "EQ", "ES", 128 * b, LQ, LS, True, True, ["EQ_0", LQ, LS])
+        for b in range(4):
+            mm(4 + b, "EQ", "ES", 128 * b, TQ, TS, True, False, ["EQ_0"] + both(TQ), 0, H)
+        for b in range(4):
+            cp("s", T.DP[:, C * b:C * b + C], T["ps%d" % b][:, 0:C], ["ps%d" % b], ["DP_%d" % b], 0.5)
+        if not swap:
+            cp("v", T.HPI[:], T[SP][:], [SP], ["HPI"])
+        cp("v", T[MK][:].indirect(T[SP][:]), T.ONE[:], [SP, "ONE"], [MK])
+        if not swap:
+            ts("v", T.NP[:], T.HPI[:], 1.0, None, A.add, None, ["HPI"], ["NP"])
+        scan(T.SEG[:, 1:UN // 2 + 1], T[MK][:, 0:UN:2], T[MK][:, 1:UN:2], 0.0, A.add, A.add, [MK], ["SEG"])
+        if not swap:
+            pair_of("NP", "HPI", "EP")
+        cp("v", T.FR[:], T.SEG[:, 0:UN // 2 + 1].indirect(T.GO[:]), ["SEG", "GO"], ["FR"])
+        if not swap:
+            cp("v", T.GP[:], T.HPI[:], ["HPI"], ["GP"])
+            cp("s", T.FP[:], T.SEG[:, 0:UN // 2 + 1].indirect(T.GP[:]), ["SEG", "GP"], ["FP"])
+
+        def part(lo, k):
+            return T[lo][:, 16 * k:16 * k + KH]
+
+        def columns_by_segment(fr, ex, even, fw, fs, win, fi, li, lj, lo, out):
+            wrap(ex, fr, [fr], halves(ex))
+            tt(T[fw][:], T[ex][:, 15:C:16], T[even][:], A.add, halves(ex) + [even], [fw])
+            ts("v", T[fs][:], T[fw][:], T.XO[:, 1:2], None, A.add, None, [fw, "XO1"], [fs])
+            cp("v", T[win][:].indirect(T[fs][:]), T.IO[:, 0:C], [fs, "IO"], [win])
+            for ks in ([[0], [1]] if out and SPLIT_LISTS else [[0, 1]]):
+                a, b = H * ks[0], H * ks[-1] + H
+                c, d = KH * ks[0], KH * ks[-1] + KH
+                nm = lambda x: [x + "h%d" % k for k in ks]
+                scan(T[fi][:, a:b], T[win][:, a:b], T.M512[:, a:b], T[fi][:, a - 1:a] if a else float(LOW), A.max, A.add,
+                     [win, "M512"] + [fi + "h0"] * (a > 0), nm(fi))
+                wrap(ex, fi, nm(fi), nm(ex), a, b)
+                ts("v", T[li][:, c:d], T[ex][:, a + 15:b:16], T.XO[:, 2:3], None, A.add, None, nm(ex) + ["XO2"], nm(li))
+                ts("v", T[lj][:, c:d], T[li][:, c:d], 511, None, A.bitwise_and, None, nm(li), nm(lj))
+                for k in ks:
+                    cp("v", part(lo, k), T[lj][:, KH * k:KH * k + KH], nm(lj), [lo + "h%d" % k])
+                if out:
+                    send(dst, "rL%d%d" % (t, ks[0]), [(part(LP, k), part(lo, k), nm(lo), nm(LP)) for k in ks])
+
+        columns_by_segment("FR", "EX", "EO", "FW", "FS", AO, "FI", "LI", "LJ", LO, swap)
+        ts("v", T.FO[:], T.FW[:], T.XO[:, 1:2], float(C), A.add, A.min, ["FW", "XO1"], ["FO"])
+        for k in range(2):
+            for b in range(4):
+                e = "v" if swap and k == 1 and b < 2 else "s"
+                cp(e, T.ZT[:, C * b + H * k:C * b + H * k + H], T.DO[:, C * b:C * b + C].indirect(part(LO, k)),
+                   ["DO_%d" % b, LO + "h%d" % k], ["ZT_%d%d" % (b, k)])
+        if t == 1:
+            cp("s", T.OL[:], T.IO[:].indirect(T.FO[:]), ["IO", "IOz", "FO"], ["OL"])
+            dma("y", "dol", [(T.ol[:], T.OL[0:128:16, :], ["OL"], [])])
+        if not swap:
+            columns_by_segment("FP", "EY", "EP", "FV", "FT", AP, "FJ", "LK", "LL", LP, False)
+
+        for k in range(2):
+            a = H * k
+            for b in range(4):
+                tt(T.Z[:, 4 * a + b:4 * (a + H):4], T.DP[:, C * b:C * b + C].indirect(part(LP, k)),
+                   T.ZT[:, C * b + a:C * b + a + H], A.add, ["DP_%d" % b, LP + "h%d" % k, "ZT_%d%d" % (b, k)],
+                   ["Z_%d%d" % (b, k)])
+            quant("ZQ", "ZS", a, a + H, "Z", slots("Z", k))
+            for b in range(4):
+                mm(b, "WQ", "WS", 128 * b, "ZQ", "ZS", True, True, ["WQ", "WS", "ZQ_%d" % a], a, a + H)
+            for b in range(4):
+                bank = "ps%d" % b
+                out, src, names = T.HP[:, HW * b + a:HW * b + a + H], T[bank][:, 0:H], ([bank], ["HP_%d%d" % (b, k)])
+                if k == 1 and b % 2 == 0:
+                    ts("v", out, src, 0.0, 0.03125, A.max, A.mult, *names)
+                else:
+                    op("s", lambda E: E.activation(out, src, AF.Relu, scale=0.03125), *names)
+        for b in range(4):
+            mm(b, "EQ", "ES", 128 * b, TQ, TS, True, False, ["EQ_0"] + both(TQ), H, C)
+        for k in range(2):
+            a, o = H * k, KH * k
+            for b in range(4):
+                cp("vs"[b % 2], T.HT[:, 4 * a + b:4 * (a + H):4], T.HP[:, HW * b:HW * b + HW].indirect(T.FO[:, o:o + KH]),
+                   ["HP_%d0" % b, "HP_%d1" % b, "HPz%d" % b, "FO"], ["HT_%d%d" % (b, k)])
+            quant("HQ", "HS", a, a + H, "HT", slots("HT", k))
+            for b in range(4):
+                mm(4 - 4 * k + b, "EQ", "ES", 128 * b, "HQ", "HS", False, True, ["EQ_0", "HQ_%d" % a], a, a + H)
+        for k in range(2):
+            a = H * k
+            for b in range(4):
+                bank = "ps%d" % (4 - 4 * k + b)
+                cp("ssss"[b] if k == 0 else "svsv"[b], T[XN][:, 4 * a + b:4 * (a + H):4], T[bank][:, 0:H],
+                   [bank], [XN + "_%d%d" % (b, k)])
+            quant(NQ, NS, a, a + H, XN, slots(XN, k))
+            if t == 1:
+                mm(4 + k, "VQ", "VS", 0, NQ, NS, True, True, ["VQ_0", NQ + "_%d" % a], a, a + H)
+            elif k == 0:
+                scores(t + 1, 0)
+
+    def store(e, out, in_, rd):
+        order(e, rd, [], False)
+        q[e].dma_start(out, in_).then_inc(T.sem["dst"], 16)
+        total["dst"] += 16
+
+    for k in range(2):
+        a = H * k
+        store("y", T.oc[:, 4 * a:4 * (a + H)], T.TQ2[:, a:a + H].bitcast(dt.uint8), ["TQ2_%d" % a])
+    for k in range(2):
+        a, bank = H * k, "ps%d" % (4 + k)
+        cp("s", T.YS[:, a:a + H], T[bank][:, 0:H], [bank], ["YS%d" % k])
+        store("s", T.y[:, a:a + H], T.YS[:, a:a + H], ["YS%d" % k])
+    for k in range(4):
+        store("y", T.osc[4 * k:4 * k + 4, :], T.TS2[32 * k:32 * k + 4, :], both("TQ2"))
+    for s in SEMAPHORES:
+        if total[s] > waited[s]:
+            q["y" if s == "dst" else "g"].wait_ge(T.sem[s], total[s])

@@ -9,10 +9,9 @@ H, KH = C // 2, K // 2
 BIG = float(2 ** 19)
 LOW = -(2 ** 20)
 STEP = [1, 2]
-SWAP_LISTS = [True, True]
-SPLIT_LISTS = True
-SCALAR_LEFT = []
-NSG, NG = 5, 3
+SCALAR_LEFT = [0, 1, 13]
+DELAY = 2
+NSG, NG = 6, 4
 
 F32, BF, I32, U16, CODE, U8 = "float32", "bfloat16", "int32", "uint16", "float8_e4m3fn_x4", "uint8"
 SCRATCH = {}
@@ -20,22 +19,20 @@ for _n, _w, _d in [
         ("X0", 4 * C, BF), ("X1", 4 * C, BF), ("X2", 4 * C, BF), ("UB", 512, BF), ("VB", 512, BF),
         ("UQ", 128, CODE), ("US", 128, U8), ("UP", 256, CODE), ("UPS", 256, U8), ("VQ", 128, CODE), ("VS", 128, U8),
         ("WQ", 512, CODE), ("WS", 512, U8), ("EB", 2048, BF), ("EQ", 512, CODE), ("ES", 512, U8),
-        ("CB", 512, BF), ("CQ", 128, CODE), ("CS", 128, U8),
+        ("CB", 512, BF), ("CQ", 128, CODE), ("CS", 128, U8), ("IA", 128, F32),
         ("I1", 128, F32), ("I2", 128, F32), ("I3", 64, F32), ("PI", 2, I32), ("PJ", 4, I32), ("PF", 4, F32),
         ("UI", 16, I32), ("UO", 16, U16), ("K16", 16, F32), ("XA", 16, F32), ("XB", 16, F32), ("XC", 16, F32),
-        ("RO", K, U16), ("XP", C, F32), ("XO", 4, F32), ("TR", 64, BF), ("QP", 3 * K, F32), ("IO", HW, F32),
-        ("ONE", C, BF), ("M512", C, F32),
+        ("RO", K, U16), ("XP", C, F32), ("XE", C, F32), ("XO", 4, F32), ("TR", 64, BF), ("QP", 3 * KH, F32),
+        ("IO", HW, F32), ("ONE", H, BF), ("M512", H, F32),
         ("TQ0", C, CODE), ("TS0", C, U8), ("TQ1", C, CODE), ("TS1", C, U8), ("TQ2", C, CODE), ("TS2", C, U8),
         ("LQ0", C, CODE), ("LS0", C, U8), ("LQ1", C, CODE), ("LS1", C, U8),
-        ("ST", C, F32), ("QF", 3 * K, F32), ("Q3", 3 * K, F32), ("QN", 3 * K, F32),
-        ("EX", C, F32), ("EY", C, F32), ("FR", C, F32), ("FP", C, F32), ("FI", C, F32), ("FJ", C, F32),
-        ("SO0", K, U16), ("SO1", K, U16), ("SP0", K, U16), ("SP1", K, U16),
+        ("ST", C, F32), ("QF", 3 * K, F32), ("Q3", 3 * K, F32), ("PN", K, F32),
+        ("EX", C, F32), ("EY", C, F32), ("FR", C, F32), ("FI", C, F32),
+        ("SO0", 32, U16), ("SO1", 32, U16), ("SP0", 32, U16), ("SP1", 32, U16),
         ("LO0", 32, U16), ("LO1", 32, U16), ("LP0", 32, U16), ("LP1", 32, U16),
-        ("FO", K, U16), ("FS", K, U16), ("FT", K, U16), ("LI", K, I32), ("LJ", K, I32), ("LK", K, I32), ("LL", K, I32),
-        ("FW", K, F32), ("FV", K, F32), ("NO", K, I32), ("HO", K, I32), ("EO", K, I32), ("GO", K, U16),
-        ("NP", K, I32), ("HPI", K, I32), ("EP", K, I32), ("GP", K, U16),
-        ("MK0", UN, BF), ("MK1", UN, BF), ("SEG", UN // 2 + 16, F32),
-        ("AO0", 2 * C, F32), ("AO1", 2 * C, F32), ("AP0", 2 * C, F32), ("AP1", 2 * C, F32),
+        ("FO", K, U16), ("FS", K, U16), ("LI", K, I32), ("LJ", K, I32),
+        ("NO", K, I32), ("HO", K, I32), ("EO", K, I32), ("GO", K, U16),
+        ("MK0", UN, BF), ("MK1", UN, BF), ("SEG", UN // 2 + 16, F32), ("AO0", 2 * C, F32), ("AO1", 2 * C, F32),
         ("DO", 4 * C, BF), ("DP", 4 * C, BF), ("ZT", 4 * C, BF), ("Z", 4 * C, BF), ("ZQ", C, CODE), ("ZS", C, U8),
         ("HP", 4 * HW, BF), ("HT", 4 * C, BF), ("HQ", C, CODE), ("HS", C, U8), ("YS", C, F32), ("OL", C, F32)]:
     SCRATCH[_n] = ("sbuf", [128, _w], _d)
@@ -47,8 +44,8 @@ for _i in range(NG):
     SCRATCH["GS%d" % _i] = ("sbuf", [128, C], U8)
 for _i in range(8):
     SCRATCH["ps%d" % _i] = ("psum", [128, 512], F32)
-SEMAPHORES = ["cv", "cs", "ct", "cg", "dx0", "dx1", "du", "dv", "dw", "dol", "sent",
-              "rT0", "rT1", "rS0", "rS1", "rL00", "rL01", "rL10", "rL11", "dst"]
+SEMAPHORES = ["cv", "cs", "ct", "cg", "dx0", "dx1", "du", "dv", "dw", "dol", "sent", "rT0", "rT1",
+              "rS00", "rS01", "rS10", "rS11", "rL00", "rL01", "rL10", "rL11", "dst"]
 
 A = AluOpType
 AF = ActivationFunctionType
@@ -153,8 +150,9 @@ def rank_program(g, core, T, topo):
         else:
             op("g", lambda E: E.iota(out, pat, base, cm, allow_small_or_imprecise_dtypes=True), [], [name])
 
-    def quant(qn, sn, a, b, tile, rd):
-        op("v", lambda E: E.quantize_mx(T[qn][:, a:b], T[sn][:, a:b], T[tile][:, 4 * a:4 * b]), rd, [qn + "_%d" % a])
+    def quant(qn, sn, a, b, tile, rd, also=()):
+        op("v", lambda E: E.quantize_mx(T[qn][:, a:b], T[sn][:, a:b], T[tile][:, 4 * a:4 * b]), rd,
+           [qn + "_%d" % c for c in (a,) + tuple(also)])
 
     def mm(bank, wq, ws, wa, xq, xs, start, stop, rd, a=0, b=C):
         bank = "ps%d" % bank
@@ -164,8 +162,8 @@ def rank_program(g, core, T, topo):
     def scan(out, d0, d1, init, o0, o1, rd, wr):
         op("v", lambda E: E.tensor_tensor_scan(out, d0, d1, init, o0, o1), rd, wr)
 
-    def wrap(dst, src, rd, wr, a=0, b=C):
-        scan(T[dst][:, a:b], T[src][:, a:b], T.XP[:, a:b], float(LOW), A.max, A.add, rd + ["XP"], wr)
+    def wrap(dst, src, rd, wr, a=0, b=C, pattern="XP"):
+        scan(T[dst][:, a:b], src, T[pattern][:, a:b], float(LOW), A.max, A.add, rd + [pattern], wr)
 
     def slots(n, k=""):
         return [n + "_%d%s" % (b, k) for b in range(4)]
@@ -176,19 +174,22 @@ def rank_program(g, core, T, topo):
     def halves(n):
         return [n + "h0", n + "h1"]
 
+    def part(name, k):
+        return T[name][:, 16 * k:16 * k + KH]
+
     def scores(t, k):
         mm(4 + k, "UQ", "US", 0, "TQ%d" % t, "TS%d" % t, True, True, ["UQ_0", "TQ%d_%d" % (t, H * k)], H * k, H * k + H)
 
     def turn(k, negate):
         a, c, w = H * k, 3 * KH * k, 3 * KH
         op("v", lambda E: E.transpose(T.ST[:, a:a + H], T["ps%d" % (4 + k)][:, 0:H]), ["ps%d" % (4 + k)], ["ST%d" % k])
+        if negate:
+            ts("v", T.PN[:, KH * k:KH * k + KH], T.ST[:, a:a + H:16], -1.0, None, A.mult, None, ["ST%d" % k], ["PN%d" % k])
         for i in range(3):
             ts("v", T.QF[:, c + i:c + w:3], T.ST[:, a + 1 + i:a + H:16], 0.0, None, A.is_gt, None,
                ["ST%d" % k], ["QF_%d%d" % (i, k)])
-        scan(T.Q3[:, c:c + w], T.QP[:, 0:w], T.QF[:, c:c + w], 1.0, A.min, A.add,
+        scan(T.Q3[:, c:c + w], T.QP[:], T.QF[:, c:c + w], 1.0, A.min, A.add,
              ["QP"] + ["QF_%d%d" % (i, k) for i in range(3)], ["Q3%d" % k])
-        if negate and any(2 * b // NB == k for b in SCALAR_LEFT):
-            ts("v", T.QN[:, c:c + w], T.Q3[:, c:c + w], -1.0, None, A.mult, None, ["Q3%d" % k], ["QN%d" % k])
 
     dma("s", "du", [(T.UB[:], T.u[:], [], ["UB"])])
     for k in range(2):
@@ -196,110 +197,131 @@ def rank_program(g, core, T, topo):
     need("y", ("dx1", 16))
     dma("y", "dw", [(T.WQ[:].bitcast(dt.uint8), T.wc[:], [], ["WQ"]), (T.WS[:], T.ws[:], [], ["WS"])])
     dma("y", "dv", [(T.VB[:], T.v[:], [], ["VB"])])
-    iota("UI", T.UI[:], [[16, 2], [32, 4], [0, 2]], 0, 0, True)
     iota("PI", T.PI[:], [[15, 2]], 0, 1, True)
+    iota("UI", T.UI[:], [[16, 2], [32, 4], [0, 2]], 0, 0, True)
     iota("K16", T.K16[:], [[1, 16]], 0, 0)
     iota("I2", T.I2[:], [[1, 8], [0, 16]], 0, 0)
     iota("I3", T.I3[:], [[1, 32], [0, 2]], 0, 0)
     iota("I1", T.I1[:], [[1, 128]], 0, -1)
     fill(T.QP[:], 1000.0, ["QP"])
-    fill(T.SEG[:, 0:16], 0.0, ["SEG"])
-    fill(T.ONE[:], 1.0, ["ONE"])
-    fill(T.QP[:, 0:3 * K:3], 1.0, ["QP"])
-    cp("v", T.UO[:], T.UI[:], ["UI"], ["UO"])
     ts("v", T.PJ[:, 0:2], T.PI[:], 15, None, A.bitwise_and, None, ["PI"], ["PJ0"])
     ts("v", T.PJ[:, 2:3], T.PI[:, 0:1], 31, None, A.bitwise_and, None, ["PI"], ["PJ2"])
     ts("v", T.PJ[:, 3:4], T.PI[:, 0:1], 5, None, A.logical_shift_right, None, ["PI"], ["PJ3"])
+    fill(T.QP[:, 0:3 * KH:3], 1.0, ["QP"])
     cp("v", T.PF[:], T.PJ[:], ["PJ0", "PJ2", "PJ3"], ["PF"])
+    cp("v", T.UO[:], T.UI[:], ["UI"], ["UO"])
     ts("v", T.XO[:, 3:4], T.PF[:, 3:4], 2.0, None, A.mult, None, ["PF"], ["XO3"])
     ts("v", T.XA[:], T.K16[:], T.PF[:, 0:1], BIG, A.is_equal, A.mult, ["K16", "PF"], ["XA"])
     ts("v", T.XB[:], T.K16[:], T.PF[:, 1:2], -2 * BIG, A.is_equal, A.mult, ["K16", "PF"], ["XB"])
     ts("v", T.RO[:], T.I2[:, 0:K], 0.0, T.PF[:, 0:1], A.mult, A.add, ["I2", "PF"], ["RO"])
-    for k, off in ((0, -BIG), (1, -BIG - 1.0), (2, -BIG + 2.0 ** 18)):
-        ts("v", T.XO[:, k:k + 1], T.XA[:, 0:1], 2.0, off, A.mult, A.add, ["XA"], ["XO%d" % k])
     tt(T.XC[:], T.XA[:], T.XB[:], A.add, ["XA", "XB"], ["XC"])
-    ts("v", T.TR[:], T.I3[:], T.PF[:, 2:3], 0.5, A.is_gt, A.mult, ["I3", "PF"], ["TR"])
+    ts("v", T.TR[:], T.I3[:], T.PF[:, 2:3], -0.5, A.is_gt, A.mult, ["I3", "PF"], ["TR"])
     for t in range(4):
         ts("v", T.CB[:, t:512:4], T.I2[:], T.XO[:, 3:4], float(t % 2), A.subtract, A.is_equal, ["I2", "XO3"], ["CB_%d" % t])
+    for k, off in ((0, -BIG), (1, -BIG - 1.0), (2, -BIG + 2.0 ** 18)):
+        op("s", lambda E: E.activation(T.XO[:, k:k + 1], T.XA[:, 0:1], AF.Identity, bias=off, scale=2.0), ["XA"], ["XO%d" % k])
+    cp("s", T.XP[:], T.XC[:].indirect(T.RO[:]), ["XC", "RO"], ["XP"])
+    op("s", lambda E: E.activation(T.IA[:], T.I1[:], AF.Abs), ["I1"], ["IA"])
     quant("UQ", "US", 0, 128, "UB", ["UB"])
     cp("s", T.UPS[:], T.US[:].indirect(T.UO[:]), ["UQ_0", "UO"], ["UPS"])
-    cp("s", T.XP[:], T.XC[:].indirect(T.RO[:]), ["XC", "RO"], ["XP"])
+    cp("s", T.XE[:], T.XP[:], ["XP"], ["XE"])
     cp("v", T.UP[:].bitcast(dt.uint32), T.UQ[:].bitcast(dt.uint32).indirect(T.UO[:]), ["UQ_0", "UO"], ["UP"])
     quant("TQ0", "TS0", 0, H, "X0", slots("X0", 0))
     scores(0, 0)
-    quant("CQ", "CS", 0, 128, "CB", slots("CB"))
     quant("TQ0", "TS0", H, C, "X0", slots("X0", 1))
+    quant("CQ", "CS", 0, 128, "CB", slots("CB"))
 
     for t in range(2):
         mate = rank ^ STEP[t]
         dst = T.cores[mate]
         buys = rank < mate
-        swap = SWAP_LISTS[t]
         n = str(t)
         XN, NQ, NS = "X" + str(t + 1), "TQ" + str(t + 1), "TS" + str(t + 1)
         TQ, TS, LQ, LS = "TQ" + n, "TS" + n, "LQ" + n, "LS" + n
-        SO, SP, LO, LP, MK, AO, AP = "SO" + n, "SP" + n, "LO" + n, "LP" + n, "MK" + n, "AO" + n, "AP" + n
+        SO, SP, LO, LP, MK, AO = "SO" + n, "SP" + n, "LO" + n, "LP" + n, "MK" + n, "AO" + n
         for h in range(2):
             mm(h, "UP", "UPS", 128 * h, TQ, TS, True, True, ["UP", "UPS"] + both(TQ))
         scores(t, 1)
         send(dst, "rT" + n, [(T[LQ][:].bitcast(dt.uint8), T[TQ][:].bitcast(dt.uint8), both(TQ), [LQ]),
                              (T[LS][:], T[TS][:], both(TQ), [LS])])
-        iota(MK, T[MK][:], [[0, UN]], 0, 0)
         if t == 0:
             iota("EB_0", T.EB[:], [[0, 2048]], 0, 0)
             for b in range(1, 4):
                 writer["EB_%d" % b] = writer["EB_0"]
+        iota(MK, T[MK][:], [[0, UN]], 0, 0)
+        if t == 0:
+            iota("ONE", T.ONE[:], [[0, H]], 1, 0)
+            iota("SEG", T.SEG[:, 0:16], [[0, 16]], 0, 0)
             iota("IO", T.IO[:, 0:C], [[1, C]], 0, 0)
-            iota("M512", T.M512[:], [[0, C]], -512, 0)
+            iota("M512", T.M512[:], [[0, H]], -512, 0)
         iota(AO, T[AO][:, 0:C], [[0, C]], LOW, 0)
-        if not swap:
-            iota(AP, T[AP][:, 0:C], [[0, C]], LOW, 0)
         if t == 0:
             for b in range(4):
                 iota("HPz%d" % b, T.HP[:, HW * b + C:HW * b + HW], [[0, HW - C]], 0, 0)
             iota("IOz", T.IO[:, C:HW], [[0, HW - C]], -1, 0)
         turn(0, not buys)
-        strict, loose = (A.is_gt, A.is_ge) if buys else (A.is_lt, A.is_le)
 
         def pack(i):
-            j = str(i % NG)
-            quant("GQ" + j, "GS" + j, 0, C, "G" + j, slots("G" + j, "l") + slots("G" + j, "r"))
-            mm(3, "CQ", "CS", 0, "GQ" + j, "GS" + j, i == 0, i == NB // 2 - 1, ["CQ_0", "GQ" + j + "_0"])
+            j, last = str(i % NG), i == NB // 2 - 1
+            rd = slots("G" + j, "l") + slots("G" + j, "r")
+            if not last:
+                quant("GQ" + j, "GS" + j, 0, C, "G" + j, rd, (H,))
+            for k in range(2):
+                if last:
+                    quant("GQ" + j, "GS" + j, H * k, H * k + H, "G" + j, rd)
+                mm(3 - k, "CQ", "CS", 0, "GQ" + j, "GS" + j, i == 0, last, ["CQ_0", "GQ%s_%d" % (j, H * k)], H * k, H * k + H)
 
         def signs(b):
             sg = "SG%d" % (b % NSG)
             for h in range(2):
-                c = 32 * b + 16 * h
+                c = 2 * b + h
+                p, pn = (T.ST[:, 16 * c:16 * c + 1], "ST") if buys else (T.PN[:, c:c + 1], "PN")
                 op("s", lambda E: E.activation(T[sg][:, h:2 * C:2], T["ps%d" % h][:, 0:C], AF.Sign,
-                                               bias=T.ST[:, c:c + 1], scale=-1.0),
-                   ["ps%d" % h, "ST%d" % (2 * b // NB)], [sg + "_%d" % h] + [sg + "d"] * (1 - h))
+                                               bias=p, scale=-1.0 if buys else 1.0),
+                   ["ps%d" % h, pn + str(2 * b // NB)], [sg + "_%d" % h] + [sg + "d"] * (1 - h))
 
+        def ties(b):
+            sg = "SG%d" % (b % NSG)
+            d = T[sg][:, 64 * b:64 * b + 64]
+            tt(d, d, T.TR[:], A.is_gt, [sg + "_0", sg + "_1", "TR"], [sg + "d"])
+
+        def weigh(b, side):
+            sg, half, gn, e = "SG%d" % (b % NSG), str(2 * b // NB), "G%d" % (b // 2 % NG), 32 * b + 32
+            for h in range(2):
+                k, c = 2 * (b % 2) + h, 3 * (2 * b + h) + 2
+                w, names = T.Q3[:, c:c + 1], ([sg + "_%d" % h, "Q3" + half], [gn + "_%d%s" % (k, side)])
+                if side == "r":
+                    if e < C:
+                        ts("v", T[gn][:, 4 * e + k:4 * C:4], T[sg][:, 2 * e + h:2 * C:2], 0.0, w, A.is_ge, A.mult, *names)
+                    continue
+                names[0].append(sg + "d")
+                if b in SCALAR_LEFT:
+                    op("s", lambda E: E.activation(T[gn][:, k:4 * e:4], T[sg][:, h:2 * e:2], AF.Relu, scale=w), *names)
+                else:
+                    ts("v", T[gn][:, k:4 * e:4], T[sg][:, h:2 * e:2], 0.0, w, A.is_gt, A.mult, *names)
+
+        last = NB - 1
+        ready = [0] * (NB // 2)
+        for b in range(NB):
+            ready[b // 2] = max(ready[b // 2], b + 1 + (DELAY if b in SCALAR_LEFT else 0))
+        packed = 0
         signs(0)
         for b in range(NB):
-            sg, half = "SG%d" % (b % NSG), str(2 * b // NB)
             if b + 1 < NB:
                 signs(b + 1)
-            d = T[sg][:, 64 * b:64 * b + 64]
-            tt(d, d, T.TR[:], A.add if buys else A.subtract, [sg + "_0", sg + "_1", "TR"], [sg + "d"])
-            if b % 2 == 0 and b > 0:
-                pack(b // 2 - 1)
-            gn, e = "G%d" % (b // 2 % NG), 32 * b + 32
-            for side in "rl":
-                for h in range(2):
-                    k, c = 2 * (b % 2) + h, 3 * (2 * b + h) + 2
-                    w = T.Q3[:, c:c + 1]
-                    eng = "s" if side == "l" and b in SCALAR_LEFT else "v"
-                    part = [gn + "_%d%s" % (k, side)]
-                    if side == "r" and e < C:
-                        ts("v", T[gn][:, 4 * e + k:4 * C:4], T[sg][:, 2 * e + h:2 * C:2], 0.0, w, loose, A.mult,
-                           [sg + "_%d" % h, "Q3" + half], part)
-                    elif side == "l" and eng == "v":
-                        ts("v", T[gn][:, k:4 * e:4], T[sg][:, h:2 * e:2], 0.0, w, strict, A.mult,
-                           [sg + "_%d" % h, sg + "d", "Q3" + half], part)
-                    elif side == "l":
-                        wn = "Q3" if buys else "QN"
-                        op("s", lambda E: E.activation(T[gn][:, k:4 * e:4], T[sg][:, h:2 * e:2], AF.Relu,
-                                                       scale=T[wn][:, c:c + 1]), [sg + "_%d" % h, sg + "d", wn + half], part)
+            if b - DELAY in SCALAR_LEFT:
+                weigh(b - DELAY, "l")
+            if not (b == last and last in SCALAR_LEFT):
+                ties(b)
+            if b == last - 1 and last in SCALAR_LEFT:
+                ties(last)
+                weigh(last, "l")
+            while packed < NB // 2 - 1 and ready[packed] <= b:
+                pack(packed)
+                packed += 1
+            weigh(b, "r")
+            if b not in SCALAR_LEFT:
+                weigh(b, "l")
             if b == 0:
                 turn(1, not buys)
                 if t > 0:
@@ -308,80 +330,63 @@ def rank_program(g, core, T, topo):
         pack(NB // 2 - 1)
         if t == 0:
             for b in range(4):
-                ts("v", T.EB[:, 512 * b + b:512 * b + 512:4], T.I1[:], 0.0, None, A.is_equal, None, ["I1"], ["EB_%d" % b])
-        wrap("EX", "ps3", ["ps3"], halves("EX"))
-        ts("v", T[SO][:], T.EX[:, 15:C:16], T.XO[:, 0:1], None, A.add, None, halves("EX") + ["XO0"], [SO])
-        send(dst, "rS" + n, [(T[SP][:], T[SO][:], [SO], [SP])])
+                op("s", lambda E: E.activation(T.EB[:, 512 * b + b:512 * b + 512:4], T.IA[:], AF.Relu, bias=1.0, scale=-1.0),
+                   ["IA"], ["EB_%d" % b])
+        for k in range(2):
+            a, ex = H * k, "EXh%d" % k
+            wrap("EX", T["ps%d" % (3 - k)][:, 0:H], ["ps%d" % (3 - k)], [ex], a, a + H)
+            ts("v", part(SO, k), T.EX[:, a + 15:a + H:16], T.XO[:, 0:1], None, A.add, None, [ex, "XO0"], [SO + "h%d" % k])
+            send(dst, "rS%d%d" % (t, k), [(part(SP, k), part(SO, k), [SO + "h%d" % k], [SP + "h%d" % k])])
         ts("v", T.NO[:], T.EX[:, 15:C:16], T.XO[:, 0:1], 1.0, A.add, A.add, halves("EX") + ["XO0"], ["NO"])
+
+        def mark(name, k):
+            cp("v", T[MK][:].indirect(part(name, k)), T.ONE[:], [name + "h%d" % k, "ONE"], [MK])
+
+        mark(SO, 0)
         if t == 0:
             quant("EQ", "ES", 0, 512, "EB", slots("EB"))
             for b in range(4):
                 mm(4 + b, "EQ", "ES", 128 * b, TQ, TS, True, True, ["EQ_0"] + both(TQ))
-
-        def pair_of(nxt, half, even):
-            ts("v", T[half][:], T[nxt][:], 1, None, A.logical_shift_right, None, [nxt], [half])
-            ts("v", T[even][:], T[nxt][:], 1, None, A.bitwise_and, None, [nxt], [even])
-
-        cp("v", T[MK][:].indirect(T[SO][:]), T.ONE[:], [SO, "ONE"], [MK])
-        pair_of("NO", "HO", "EO")
-        if t == 1:
-            quant("VQ", "VS", 0, 128, "VB", ["VB"])
+        ts("v", T.HO[:], T.NO[:], 1, None, A.logical_shift_right, None, ["NO"], ["HO"])
+        ts("v", T.EO[:], T.NO[:], 1, None, A.bitwise_and, None, ["NO"], ["EO"])
+        mark(SO, 1)
         cp("v", T.GO[:], T.HO[:], ["HO"], ["GO"])
+        mark(SP, 0)
+        tt(T.XE[:, 15:C:16], T.XP[:, 15:C:16], T.EO[:], A.add, ["XP", "EO"], ["XE"])
         for b in range(4):
             cp("s", T.DO[:, C * b:C * b + C], T["ps%d" % (4 + b)][:, 0:C], ["ps%d" % (4 + b)], ["DO_%d" % b], 0.5)
         for b in range(4):
             mm(b, "EQ", "ES", 128 * b, LQ, LS, True, True, ["EQ_0", LQ, LS])
         for b in range(4):
             mm(4 + b, "EQ", "ES", 128 * b, TQ, TS, True, False, ["EQ_0"] + both(TQ), 0, H)
+        mark(SP, 1)
+        scan(T.SEG[:, 1:UN // 2 + 1], T[MK][:, 0:UN:2], T[MK][:, 1:UN:2], 0.0, A.add, A.add, [MK], ["SEG"])
+        for k in range(2):
+            cp("vs"[k], T.FR[:, H * k:H * k + H], T.SEG[:, 0:UN // 2 + 1].indirect(T.GO[:, KH * k:KH * k + KH]),
+               ["SEG", "GO"], ["FRh%d" % k])
         for b in range(4):
             cp("s", T.DP[:, C * b:C * b + C], T["ps%d" % b][:, 0:C], ["ps%d" % b], ["DP_%d" % b], 0.5)
-        if not swap:
-            cp("v", T.HPI[:], T[SP][:], [SP], ["HPI"])
-        cp("v", T[MK][:].indirect(T[SP][:]), T.ONE[:], [SP, "ONE"], [MK])
-        if not swap:
-            ts("v", T.NP[:], T.HPI[:], 1.0, None, A.add, None, ["HPI"], ["NP"])
-        scan(T.SEG[:, 1:UN // 2 + 1], T[MK][:, 0:UN:2], T[MK][:, 1:UN:2], 0.0, A.add, A.add, [MK], ["SEG"])
-        if not swap:
-            pair_of("NP", "HPI", "EP")
-        cp("v", T.FR[:], T.SEG[:, 0:UN // 2 + 1].indirect(T.GO[:]), ["SEG", "GO"], ["FR"])
-        if not swap:
-            cp("v", T.GP[:], T.HPI[:], ["HPI"], ["GP"])
-            cp("s", T.FP[:], T.SEG[:, 0:UN // 2 + 1].indirect(T.GP[:]), ["SEG", "GP"], ["FP"])
-
-        def part(lo, k):
-            return T[lo][:, 16 * k:16 * k + KH]
-
-        def columns_by_segment(fr, ex, even, fw, fs, win, fi, li, lj, lo, out):
-            wrap(ex, fr, [fr], halves(ex))
-            tt(T[fw][:], T[ex][:, 15:C:16], T[even][:], A.add, halves(ex) + [even], [fw])
-            ts("v", T[fs][:], T[fw][:], T.XO[:, 1:2], None, A.add, None, [fw, "XO1"], [fs])
-            cp("v", T[win][:].indirect(T[fs][:]), T.IO[:, 0:C], [fs, "IO"], [win])
-            for ks in ([[0], [1]] if out and SPLIT_LISTS else [[0, 1]]):
-                a, b = H * ks[0], H * ks[-1] + H
-                c, d = KH * ks[0], KH * ks[-1] + KH
-                nm = lambda x: [x + "h%d" % k for k in ks]
-                scan(T[fi][:, a:b], T[win][:, a:b], T.M512[:, a:b], T[fi][:, a - 1:a] if a else float(LOW), A.max, A.add,
-                     [win, "M512"] + [fi + "h0"] * (a > 0), nm(fi))
-                wrap(ex, fi, nm(fi), nm(ex), a, b)
-                ts("v", T[li][:, c:d], T[ex][:, a + 15:b:16], T.XO[:, 2:3], None, A.add, None, nm(ex) + ["XO2"], nm(li))
-                ts("v", T[lj][:, c:d], T[li][:, c:d], 511, None, A.bitwise_and, None, nm(li), nm(lj))
-                for k in ks:
-                    cp("v", part(lo, k), T[lj][:, KH * k:KH * k + KH], nm(lj), [lo + "h%d" % k])
-                if out:
-                    send(dst, "rL%d%d" % (t, ks[0]), [(part(LP, k), part(lo, k), nm(lo), nm(LP)) for k in ks])
-
-        columns_by_segment("FR", "EX", "EO", "FW", "FS", AO, "FI", "LI", "LJ", LO, swap)
-        ts("v", T.FO[:], T.FW[:], T.XO[:, 1:2], float(C), A.add, A.min, ["FW", "XO1"], ["FO"])
+        wrap("EY", T.FR[:], halves("FR"), ["EY"], pattern="XE")
+        ts("v", T.FS[:], T.EY[:, 15:C:16], T.XO[:, 1:2], None, A.add, None, ["EY", "XO1"], ["FS"])
+        cp("v", T[AO][:].indirect(T.FS[:]), T.IO[:, 0:C], ["FS", "IO"], [AO])
+        for k in range(2):
+            a, c, hk = H * k, KH * k, "h%d" % k
+            scan(T.FI[:, a:a + H], T[AO][:, a:a + H], T.M512[:], T.FI[:, a - 1:a] if k else float(LOW), A.max, A.add,
+                 [AO, "M512"] + ["FIh0"] * k, ["FI" + hk])
+            wrap("EX", T.FI[:, a:a + H], ["FI" + hk], ["EX" + hk], a, a + H)
+            ts("v", T.LI[:, c:c + KH], T.EX[:, a + 15:a + H:16], T.XO[:, 2:3], None, A.add, None, ["EX" + hk, "XO2"], ["LI" + hk])
+            ts("v", T.LJ[:, c:c + KH], T.LI[:, c:c + KH], 511, None, A.bitwise_and, None, ["LI" + hk], ["LJ" + hk])
+            cp("v", part(LO, k), T.LJ[:, c:c + KH], ["LJ" + hk], [LO + hk])
+            send(dst, "rL%d%d" % (t, k), [(part(LP, k), part(LO, k), [LO + hk], [LP + hk])])
+        ts("v", T.FO[:], T.EY[:, 15:C:16], T.XO[:, 1:2], float(C), A.add, A.min, ["EY", "XO1"], ["FO"])
         for k in range(2):
             for b in range(4):
-                e = "v" if swap and k == 1 and b < 2 else "s"
-                cp(e, T.ZT[:, C * b + H * k:C * b + H * k + H], T.DO[:, C * b:C * b + C].indirect(part(LO, k)),
-                   ["DO_%d" % b, LO + "h%d" % k], ["ZT_%d%d" % (b, k)])
+                cp("v" if k == 1 and b < 2 else "s", T.ZT[:, C * b + H * k:C * b + H * k + H],
+                   T.DO[:, C * b:C * b + C].indirect(part(LO, k)), ["DO_%d" % b, LO + "h%d" % k], ["ZT_%d%d" % (b, k)])
         if t == 1:
+            quant("VQ", "VS", 0, 128, "VB", ["VB"])
             cp("s", T.OL[:], T.IO[:].indirect(T.FO[:]), ["IO", "IOz", "FO"], ["OL"])
             dma("y", "dol", [(T.ol[:], T.OL[0:128:16, :], ["OL"], [])])
-        if not swap:
-            columns_by_segment("FP", "EY", "EP", "FV", "FT", AP, "FJ", "LK", "LL", LP, False)
 
         for k in range(2):
             a = H * k
@@ -426,15 +431,25 @@ def rank_program(g, core, T, topo):
         q[e].dma_start(out, in_).then_inc(T.sem["dst"], 16)
         total["dst"] += 16
 
-    for k in range(2):
-        a = H * k
-        store("y", T.oc[:, 4 * a:4 * (a + H)], T.TQ2[:, a:a + H].bitcast(dt.uint8), ["TQ2_%d" % a])
-    for k in range(2):
+    def codes(k):
+        store("y", T.oc[:, 4 * H * k:4 * H * (k + 1)], T.TQ2[:, H * k:H * (k + 1)].bitcast(dt.uint8), ["TQ2_%d" % (H * k)])
+
+    def scales(e, k):
+        store(e, T.osc[4 * k:4 * k + 4, :], T.TS2[32 * k:32 * k + 4, :], both("TQ2"))
+
+    def result(k):
         a, bank = H * k, "ps%d" % (4 + k)
-        cp("s", T.YS[:, a:a + H], T[bank][:, 0:H], [bank], ["YS%d" % k])
+        cp("sv"[k], T.YS[:, a:a + H], T[bank][:, 0:H], [bank], ["YS%d" % k])
         store("s", T.y[:, a:a + H], T.YS[:, a:a + H], ["YS%d" % k])
-    for k in range(4):
-        store("y", T.osc[4 * k:4 * k + 4, :], T.TS2[32 * k:32 * k + 4, :], both("TQ2"))
+
+    codes(0)
+    result(0)
+    codes(1)
+    scales("s", 0)
+    result(1)
+    scales("y", 1)
+    scales("y", 2)
+    scales("s", 3)
     for s in SEMAPHORES:
         if total[s] > waited[s]:
             q["y" if s == "dst" else "g"].wait_ge(T.sem[s], total[s])

@@ -5,33 +5,44 @@ K = C // 16
 NB = C // 32
 UN = 4 * C
 HW = C + 16
-H, KH = C // 2, K // 2
 BIG = float(2 ** 19)
 LOW = -(2 ** 20)
+AGE = 512.0
 STEP = [1, 2]
+TC = [[0, 224, C], [0, 224, C], [0, 224, C]]
+UC = [0, 160, C]
+ZC = [0, 224, C]
+EARLY = [0, 0]
 SCALAR_LEFT = [0, 1, 13]
+DIRECT = {}
 DELAY = 2
+BEFORE = [2, 5]
+OWN_ON = ["ssss", "vvss"]
+RELU_ON = ["ssss", "vsvs"]
+PICK_ON = ["vsvs", "vsvs"]
+STATE_ON = ["ssss", "svsv"]
 NSG, NG = 6, 4
+P, Q = [0, 1, 2, 3], [4, 5, 6, 7]
 
 F32, BF, I32, U16, CODE, U8 = "float32", "bfloat16", "int32", "uint16", "float8_e4m3fn_x4", "uint8"
 SCRATCH = {}
 for _n, _w, _d in [
         ("X0", 4 * C, BF), ("X1", 4 * C, BF), ("X2", 4 * C, BF), ("UB", 512, BF), ("VB", 512, BF),
-        ("UQ", 128, CODE), ("US", 128, U8), ("UP", 256, CODE), ("UPS", 256, U8), ("VQ", 128, CODE), ("VS", 128, U8),
-        ("WQ", 512, CODE), ("WS", 512, U8), ("EB", 2048, BF), ("EQ", 512, CODE), ("ES", 512, U8),
-        ("CB", 512, BF), ("CQ", 128, CODE), ("CS", 128, U8), ("IA", 128, F32),
-        ("I1", 128, F32), ("I2", 128, F32), ("I3", 64, F32), ("PI", 2, I32), ("PJ", 4, I32), ("PF", 4, F32),
-        ("UI", 16, I32), ("UO", 16, U16), ("K16", 16, F32), ("XA", 16, F32), ("XB", 16, F32), ("XC", 16, F32),
-        ("RO", K, U16), ("XP", C, F32), ("XE", C, F32), ("XO", 4, F32), ("TR", 64, BF), ("QP", 3 * KH, F32),
-        ("IO", HW, F32), ("ONE", H, BF), ("M512", H, F32),
+        ("UQ", 128, CODE), ("US", 128, U8), ("UP", 384, CODE), ("UPS", 384, U8), ("VQ", 128, CODE), ("VS", 128, U8),
+        ("WQ", 512, CODE), ("WS", 512, U8), ("EB", 516, BF), ("EQ", 512, CODE), ("ES", 512, U8),
+        ("CB", 512, BF), ("CQ", 128, CODE), ("CS", 128, U8),
+        ("I2", 512, BF), ("I3", 64, F32), ("PI", 2, I32), ("PJ", 6, I32), ("PF", 6, F32),
+        ("UI", 24, F32), ("UO", 24, U16), ("K16", 16, F32), ("XA", 16, F32), ("XB", 16, F32), ("XC", 16, F32),
+        ("XD", 16, F32), ("XF", 16, F32), ("XG", 16, F32),
+        ("RO", K, U16), ("XP", C, F32), ("XE", C, F32), ("XH", C, F32), ("XO", 8, F32), ("TR", 64, BF),
+        ("QP", C // 4, F32), ("IO", HW, F32), ("ONE", 516, BF),
         ("TQ0", C, CODE), ("TS0", C, U8), ("TQ1", C, CODE), ("TS1", C, U8), ("TQ2", C, CODE), ("TS2", C, U8),
         ("LQ0", C, CODE), ("LS0", C, U8), ("LQ1", C, CODE), ("LS1", C, U8),
-        ("ST", C, F32), ("QF", 3 * K, F32), ("Q3", 3 * K, F32), ("PN", K, F32),
-        ("EX", C, F32), ("EY", C, F32), ("FR", C, F32), ("FI", C, F32),
+        ("ST", C, F32), ("QF", C // 4, F32), ("Q4", C // 4, BF), ("QS", K, F32), ("PN", K, F32),
+        ("EX", C, F32), ("EY", C, F32), ("EZ", C, F32), ("FR", C, F32),
         ("SO0", 32, U16), ("SO1", 32, U16), ("SP0", 32, U16), ("SP1", 32, U16),
         ("LO0", 32, U16), ("LO1", 32, U16), ("LP0", 32, U16), ("LP1", 32, U16),
-        ("FO", K, U16), ("FS", K, U16), ("LI", K, I32), ("LJ", K, I32),
-        ("NO", K, I32), ("HO", K, I32), ("EO", K, I32), ("GO", K, U16),
+        ("FO", K, U16), ("FS", K, U16), ("LI", K, I32), ("LJ", K, I32), ("EO", K, F32), ("GO", K, U16),
         ("MK0", UN, BF), ("MK1", UN, BF), ("SEG", UN // 2 + 16, F32), ("AO0", 2 * C, F32), ("AO1", 2 * C, F32),
         ("DO", 4 * C, BF), ("DP", 4 * C, BF), ("ZT", 4 * C, BF), ("Z", 4 * C, BF), ("ZQ", C, CODE), ("ZS", C, U8),
         ("HP", 4 * HW, BF), ("HT", 4 * C, BF), ("HQ", C, CODE), ("HS", C, U8), ("YS", C, F32), ("OL", C, F32)]:
@@ -44,11 +55,16 @@ for _i in range(NG):
     SCRATCH["GS%d" % _i] = ("sbuf", [128, C], U8)
 for _i in range(8):
     SCRATCH["ps%d" % _i] = ("psum", [128, 512], F32)
-SEMAPHORES = ["cv", "cs", "ct", "cg", "dx0", "dx1", "du", "dv", "dw", "dol", "sent", "rT0", "rT1",
-              "rS00", "rS01", "rS10", "rS11", "rL00", "rL01", "rL10", "rL11", "dst"]
+SEMAPHORES = (["cv", "cs", "ct", "cg", "dx0", "dx1", "du", "dv", "dw", "dol", "sent", "rT0", "rT1", "dst"]
+              + ["rS%d%d" % (_t, _k) for _t in range(2) for _k in range(len(UC) - 1)]
+              + ["rL%d%d" % (_t, _k) for _t in range(2) for _k in range(len(ZC) - 1)])
 
 A = AluOpType
 AF = ActivationFunctionType
+
+
+def runs(edges):
+    return list(zip(edges[:-1], edges[1:]))
 
 
 def rank_program(g, core, T, topo):
@@ -74,7 +90,7 @@ def rank_program(g, core, T, topo):
     def order(e, rd, wr, acc):
         toks = []
         for k in rd:
-            toks += writer.get(k, [])
+            toks += writer[k]
             if k.startswith("ps"):
                 toks += [t for f, t in readers.get(k, []) if f != e]
         for k in wr:
@@ -133,13 +149,14 @@ def rank_program(g, core, T, topo):
     def tt(out, a, b, o, rd, wr):
         op("v", lambda E: E.tensor_tensor(out, a, b, o), rd, wr)
 
-    def cp(e, out, in_, rd, wr, scale=None):
+    def act(out, in_, f, rd, wr, **kw):
+        op("s", lambda E: E.activation(out, in_, f, **kw), rd, wr)
+
+    def cp(e, out, in_, rd, wr):
         if e == "v":
             op(e, lambda E: E.tensor_copy(out, in_), rd, wr)
-        elif scale is None:
-            op(e, lambda E: E.activation(out, in_, AF.Copy), rd, wr)
         else:
-            op(e, lambda E: E.activation(out, in_, AF.Copy, scale=scale), rd, wr)
+            act(out, in_, AF.Copy, rd, wr)
 
     def fill(out, val, wr):
         op("v", lambda E: E.memset(out, val), [], wr)
@@ -150,9 +167,8 @@ def rank_program(g, core, T, topo):
         else:
             op("g", lambda E: E.iota(out, pat, base, cm, allow_small_or_imprecise_dtypes=True), [], [name])
 
-    def quant(qn, sn, a, b, tile, rd, also=()):
-        op("v", lambda E: E.quantize_mx(T[qn][:, a:b], T[sn][:, a:b], T[tile][:, 4 * a:4 * b]), rd,
-           [qn + "_%d" % c for c in (a,) + tuple(also)])
+    def quant(qn, sn, a, b, src, rd, wr):
+        op("v", lambda E: E.quantize_mx(T[qn][:, a:b], T[sn][:, a:b], src), rd, wr)
 
     def mm(bank, wq, ws, wa, xq, xs, start, stop, rd, a=0, b=C):
         bank = "ps%d" % bank
@@ -162,74 +178,104 @@ def rank_program(g, core, T, topo):
     def scan(out, d0, d1, init, o0, o1, rd, wr):
         op("v", lambda E: E.tensor_tensor_scan(out, d0, d1, init, o0, o1), rd, wr)
 
-    def wrap(dst, src, rd, wr, a=0, b=C, pattern="XP"):
-        scan(T[dst][:, a:b], src, T[pattern][:, a:b], float(LOW), A.max, A.add, rd + [pattern], wr)
+    def wrap(dst, src, rd, wr, a, b, pattern, init=float(LOW)):
+        scan(T[dst][:, a:b], src, T[pattern][:, a:b], init, A.max, A.add, rd + [pattern], wr)
 
     def slots(n, k=""):
         return [n + "_%d%s" % (b, k) for b in range(4)]
 
-    def both(n):
-        return [n + "_0", n + "_%d" % H]
+    def parts(n, edges):
+        return [n + "_%d" % a for a in edges[:-1]]
 
-    def halves(n):
-        return [n + "h0", n + "h1"]
+    def ps(bank):
+        return "ps%d" % bank
 
-    def part(name, k):
-        return T[name][:, 16 * k:16 * k + KH]
+    def unpack(banks, qn, sn, rd, start, stop, a=0, b=C):
+        for i in range(4):
+            mm(banks[i], "EQ", "ES", 128 * i, qn, sn, start, stop, ["EQ_%d" % i] + rd, a, b)
 
     def scores(t, k):
-        mm(4 + k, "UQ", "US", 0, "TQ%d" % t, "TS%d" % t, True, True, ["UQ_0", "TQ%d_%d" % (t, H * k)], H * k, H * k + H)
+        a, b = runs(TC[t])[k]
+        tq, tsc, banks = "TQ%d" % t, "TS%d" % t, (P, Q)[k]
+        rd = ["UP", "UPS"] + parts(tq, TC[t][:k + 2])
+        todo = [(banks[h], 128 * h, 0) for h in range(2) if k or EARLY[t]]
+        todo.insert(2 * k, (banks[2], 256, a))
+        if k and DIRECT:
+            todo += [((P, Q)[h][3], 128 * h, 0) for h in range(2)]
+        for bank, wa, a0 in todo:
+            mm(bank, "UP", "UPS", wa, tq, tsc, True, True, rd, a0, b)
 
-    def turn(k, negate):
-        a, c, w = H * k, 3 * KH * k, 3 * KH
-        op("v", lambda E: E.transpose(T.ST[:, a:a + H], T["ps%d" % (4 + k)][:, 0:H]), ["ps%d" % (4 + k)], ["ST%d" % k])
+    def turn(t, k, negate):
+        a, b = runs(TC[t])[k]
+        bank = ps((P, Q)[k][2])
+        op("v", lambda E: E.transpose(T.ST[:, a:b], T[bank][:, 0:b - a]), [bank], ["ST%d" % k])
         if negate:
-            ts("v", T.PN[:, KH * k:KH * k + KH], T.ST[:, a:a + H:16], -1.0, None, A.mult, None, ["ST%d" % k], ["PN%d" % k])
-        for i in range(3):
-            ts("v", T.QF[:, c + i:c + w:3], T.ST[:, a + 1 + i:a + H:16], 0.0, None, A.is_gt, None,
-               ["ST%d" % k], ["QF_%d%d" % (i, k)])
-        scan(T.Q3[:, c:c + w], T.QP[:], T.QF[:, c:c + w], 1.0, A.min, A.add,
-             ["QP"] + ["QF_%d%d" % (i, k) for i in range(3)], ["Q3%d" % k])
+            act(T.PN[:, a // 16:b // 16], T.ST[:, a:b:16], AF.Copy, ["ST%d" % k], ["PN%d" % k], scale=-1.0)
+        ts("v", T.QF[:, a // 4:b // 4], T.ST[:, a:b:4], 0.0, None, A.is_gt, None, ["ST%d" % k], ["QF%d" % k])
+        scan(T.Q4[:, a // 4:b // 4], T.QP[:, a // 4:b // 4], T.QF[:, a // 4:b // 4], 1.0, A.min, A.add,
+             ["QP", "QF%d" % k], ["Q4%d" % k])
 
     dma("s", "du", [(T.UB[:], T.u[:], [], ["UB"])])
-    for k in range(2):
-        dma("y", "dx%d" % k, [(T.X0[:, 4 * H * k:4 * H * k + 4 * H], T.x[:, 4 * H * k:4 * H * k + 4 * H], [], slots("X0", k))])
+    for k, (a, b) in enumerate(runs(TC[0])):
+        dma("y", "dx%d" % k, [(T.X0[:, 4 * a:4 * b], T.x[:, 4 * a:4 * b], [], slots("X0", k))])
     need("y", ("dx1", 16))
     dma("y", "dw", [(T.WQ[:].bitcast(dt.uint8), T.wc[:], [], ["WQ"]), (T.WS[:], T.ws[:], [], ["WS"])])
     dma("y", "dv", [(T.VB[:], T.v[:], [], ["VB"])])
     iota("PI", T.PI[:], [[15, 2]], 0, 1, True)
-    iota("UI", T.UI[:], [[16, 2], [32, 4], [0, 2]], 0, 0, True)
+    iota("UI", T.UI[:, 0:16], [[16, 2], [32, 4], [0, 2]], 0, 0)
     iota("K16", T.K16[:], [[1, 16]], 0, 0)
-    iota("I2", T.I2[:], [[1, 8], [0, 16]], 0, 0)
     iota("I3", T.I3[:], [[1, 32], [0, 2]], 0, 0)
-    iota("I1", T.I1[:], [[1, 128]], 0, -1)
+    iota("I2", T.I2[:], [[1, 8], [0, 32], [-1, 2]], 0, 0)
     fill(T.QP[:], 1000.0, ["QP"])
+    fill(T.QP[:, 1:C // 4:4], 1.0, ["QP"])
     ts("v", T.PJ[:, 0:2], T.PI[:], 15, None, A.bitwise_and, None, ["PI"], ["PJ0"])
     ts("v", T.PJ[:, 2:3], T.PI[:, 0:1], 31, None, A.bitwise_and, None, ["PI"], ["PJ2"])
-    ts("v", T.PJ[:, 3:4], T.PI[:, 0:1], 5, None, A.logical_shift_right, None, ["PI"], ["PJ3"])
-    fill(T.QP[:, 0:3 * KH:3], 1.0, ["QP"])
-    cp("v", T.PF[:], T.PJ[:], ["PJ0", "PJ2", "PJ3"], ["PF"])
-    cp("v", T.UO[:], T.UI[:], ["UI"], ["UO"])
-    ts("v", T.XO[:, 3:4], T.PF[:, 3:4], 2.0, None, A.mult, None, ["PF"], ["XO3"])
+    ts("v", T.PJ[:, 3:4], T.PI[:, 0:1], 4, 6, A.logical_shift_right, A.bitwise_and, ["PI"], ["PJ3"])
+    ts("v", T.PJ[:, 4:5], T.PI[:, 0:1], 2, 3, A.logical_shift_right, A.bitwise_and, ["PI"], ["PJ4"])
+    ts("v", T.PJ[:, 5:6], T.PI[:, 0:1], 8, None, A.bitwise_and, None, ["PI"], ["PJ5"])
+    cp("v", T.UO[:, 0:16], T.UI[:, 0:16], ["UI"], ["UO0"])
+    cp("v", T.PF[:], T.PJ[:], ["PJ0", "PJ2", "PJ3", "PJ4", "PJ5"], ["PF"])
+    ts("v", T.UO[:, 16:24], T.K16[:, 0:8], 16.0, T.PF[:, 4:5], A.mult, A.add, ["K16", "PF"], ["UO1"])
     ts("v", T.XA[:], T.K16[:], T.PF[:, 0:1], BIG, A.is_equal, A.mult, ["K16", "PF"], ["XA"])
     ts("v", T.XB[:], T.K16[:], T.PF[:, 1:2], -2 * BIG, A.is_equal, A.mult, ["K16", "PF"], ["XB"])
-    ts("v", T.RO[:], T.I2[:, 0:K], 0.0, T.PF[:, 0:1], A.mult, A.add, ["I2", "PF"], ["RO"])
+    ts("v", T.RO[:], T.QP[:, 0:K], 0.0, T.PF[:, 0:1], A.mult, A.add, ["QP", "PF"], ["RO"])
     tt(T.XC[:], T.XA[:], T.XB[:], A.add, ["XA", "XB"], ["XC"])
-    ts("v", T.TR[:], T.I3[:], T.PF[:, 2:3], -0.5, A.is_gt, A.mult, ["I3", "PF"], ["TR"])
-    for t in range(4):
-        ts("v", T.CB[:, t:512:4], T.I2[:], T.XO[:, 3:4], float(t % 2), A.subtract, A.is_equal, ["I2", "XO3"], ["CB_%d" % t])
-    for k, off in ((0, -BIG), (1, -BIG - 1.0), (2, -BIG + 2.0 ** 18)):
-        op("s", lambda E: E.activation(T.XO[:, k:k + 1], T.XA[:, 0:1], AF.Identity, bias=off, scale=2.0), ["XA"], ["XO%d" % k])
     cp("s", T.XP[:], T.XC[:].indirect(T.RO[:]), ["XC", "RO"], ["XP"])
-    op("s", lambda E: E.activation(T.IA[:], T.I1[:], AF.Abs), ["I1"], ["IA"])
-    quant("UQ", "US", 0, 128, "UB", ["UB"])
-    cp("s", T.UPS[:], T.US[:].indirect(T.UO[:]), ["UQ_0", "UO"], ["UPS"])
-    cp("s", T.XE[:], T.XP[:], ["XP"], ["XE"])
-    cp("v", T.UP[:].bitcast(dt.uint32), T.UQ[:].bitcast(dt.uint32).indirect(T.UO[:]), ["UQ_0", "UO"], ["UP"])
-    quant("TQ0", "TS0", 0, H, "X0", slots("X0", 0))
+    quant("UQ", "US", 0, 128, T.UB[:], ["UB"], ["UQ"])
+    cp("s", T.UPS[:], T.US[:].indirect(T.UO[:]), ["UQ", "UO0", "UO1"], ["UPS"])
+    ts("v", T.TR[:], T.I3[:], T.PF[:, 2:3], -0.5, A.is_gt, A.mult, ["I3", "PF"], ["TR"])
+    cp("v", T.UP[:].bitcast(dt.uint32), T.UQ[:].bitcast(dt.uint32).indirect(T.UO[:]), ["UQ", "UO0", "UO1"], ["UP"])
+    act(T.XO[:, 6:7], T.XA[:, 0:1], AF.Identity, ["XA"], ["XO6"], bias=-BIG - 1.0, scale=2.0)
+    act(T.XO[:, 0:5], T.K16[:, 0:5], AF.Identity, ["K16", "XO6"], ["XO"], bias=T.XO[:, 6:7], scale=0.5)
+    act(T.XO[:, 5:6], T.XC[:, 15:16], AF.Identity, ["XC", "XO"], ["XO5"], bias=T.XO[:, 4:5])
+    for j in range(NG):
+        for side in "lrd":
+            for k in slots("G%d" % j, side):
+                writer[k] = []
+
+    def state(t, k):
+        a, b = runs(TC[t])[k]
+        quant("TQ%d" % t, "TS%d" % t, a, b, T["X%d" % t][:, 4 * a:4 * b], slots("X%d" % t, k), ["TQ%d_%d" % (t, a)])
+
+    def signs(t, b, side="ab"):
+        sg, buys, cut = "SG%d" % (b % NSG), rank < rank ^ STEP[t], TC[t][1]
+        a0, a1 = cut if side == "b" else 0, cut if side == "a" else DIRECT.get(b, C)
+        for h in range(2):
+            c, bank = 2 * b + h, ps((P if side == "a" else Q)[h])
+            p, pn = (T.ST[:, 16 * c:16 * c + 1], "ST") if buys else (T.PN[:, c:c + 1], "PN")
+            act(T[sg][:, 2 * a0 + h:2 * a1:2], T[bank][:, a0:a1], AF.Sign, [bank, pn + str(int(32 * b >= cut))],
+                [sg + "_%d%s" % (h, s) for s in side] + [sg + "d"] * ((1 - h) * ("a" in side)),
+                bias=p, scale=-1.0 if buys else 1.0)
+
+    state(0, 0)
     scores(0, 0)
-    quant("TQ0", "TS0", H, C, "X0", slots("X0", 1))
-    quant("CQ", "CS", 0, 128, "CB", slots("CB"))
+    state(0, 1)
+    turn(0, 0, rank > rank ^ STEP[0])
+    for b in range(EARLY[0]):
+        signs(0, b, "a")
+    ts("v", T.CB[:], T.I2[:], T.PF[:, 3:4], None, A.is_equal, None, ["I2", "PF"], ["CB"])
+    ts("v", T.XD[:], T.K16[:], T.PF[:, 5:6], 8.0, A.add, A.is_equal, ["K16", "PF"], ["XD"])
+    quant("CQ", "CS", 0, 128, T.CB[:], ["CB"], ["CQ"])
 
     for t in range(2):
         mate = rank ^ STEP[t]
@@ -239,64 +285,64 @@ def rank_program(g, core, T, topo):
         XN, NQ, NS = "X" + str(t + 1), "TQ" + str(t + 1), "TS" + str(t + 1)
         TQ, TS, LQ, LS = "TQ" + n, "TS" + n, "LQ" + n, "LS" + n
         SO, SP, LO, LP, MK, AO = "SO" + n, "SP" + n, "LO" + n, "LP" + n, "MK" + n, "AO" + n
-        for h in range(2):
-            mm(h, "UP", "UPS", 128 * h, TQ, TS, True, True, ["UP", "UPS"] + both(TQ))
+        whole = parts(TQ, TC[t])
         scores(t, 1)
-        send(dst, "rT" + n, [(T[LQ][:].bitcast(dt.uint8), T[TQ][:].bitcast(dt.uint8), both(TQ), [LQ]),
-                             (T[LS][:], T[TS][:], both(TQ), [LS])])
-        if t == 0:
-            iota("EB_0", T.EB[:], [[0, 2048]], 0, 0)
-            for b in range(1, 4):
-                writer["EB_%d" % b] = writer["EB_0"]
+        send(dst, "rT" + n, [(T[LQ][:].bitcast(dt.uint8), T[TQ][:].bitcast(dt.uint8), whole, [LQ]),
+                             (T[LS][:], T[TS][:], whole, [LS])])
         iota(MK, T[MK][:], [[0, UN]], 0, 0)
         if t == 0:
-            iota("ONE", T.ONE[:], [[0, H]], 1, 0)
+            iota("ONE", T.ONE[:], [[0, 516]], 1, 0)
+            op("g", lambda E: E.affine_select(T.EB[:], T.ONE[:], [[1, 516]], A.is_equal, 0.0, -3, -4), ["ONE"], ["EB"])
+            op("g", lambda E: E.affine_select(T.XE[:], T.XP[:], [[0, C]], A.is_equal, 0.0, 0, 0), ["XP"], ["XE"])
             iota("SEG", T.SEG[:, 0:16], [[0, 16]], 0, 0)
             iota("IO", T.IO[:, 0:C], [[1, C]], 0, 0)
-            iota("M512", T.M512[:], [[0, H]], -512, 0)
         iota(AO, T[AO][:, 0:C], [[0, C]], LOW, 0)
         if t == 0:
             for b in range(4):
                 iota("HPz%d" % b, T.HP[:, HW * b + C:HW * b + HW], [[0, HW - C]], 0, 0)
             iota("IOz", T.IO[:, C:HW], [[0, HW - C]], -1, 0)
-        turn(0, not buys)
 
         def pack(i):
             j, last = str(i % NG), i == NB // 2 - 1
-            rd = slots("G" + j, "l") + slots("G" + j, "r")
+            gq, gs, rd = "GQ" + j, "GS" + j, [k for side in "lrd" for k in slots("G" + j, side)]
             if not last:
-                quant("GQ" + j, "GS" + j, 0, C, "G" + j, rd, (H,))
-            for k in range(2):
+                quant(gq, gs, 0, C, T["G" + j][:], rd, parts(gq, UC))
+            for k, (a, b) in enumerate(runs(UC)):
                 if last:
-                    quant("GQ" + j, "GS" + j, H * k, H * k + H, "G" + j, rd)
-                mm(3 - k, "CQ", "CS", 0, "GQ" + j, "GS" + j, i == 0, last, ["CQ_0", "GQ%s_%d" % (j, H * k)], H * k, H * k + H)
-
-        def signs(b):
-            sg = "SG%d" % (b % NSG)
-            for h in range(2):
-                c = 2 * b + h
-                p, pn = (T.ST[:, 16 * c:16 * c + 1], "ST") if buys else (T.PN[:, c:c + 1], "PN")
-                op("s", lambda E: E.activation(T[sg][:, h:2 * C:2], T["ps%d" % h][:, 0:C], AF.Sign,
-                                               bias=p, scale=-1.0 if buys else 1.0),
-                   ["ps%d" % h, pn + str(2 * b // NB)], [sg + "_%d" % h] + [sg + "d"] * (1 - h))
+                    quant(gq, gs, a, b, T["G" + j][:, 4 * a:4 * b], rd, [gq + "_%d" % a])
+                mm(P[k], "CQ", "CS", 0, gq, gs, i == 0, last, ["CQ", gq + "_%d" % a], a, b)
 
         def ties(b):
-            sg = "SG%d" % (b % NSG)
+            sg, s = "SG%d" % (b % NSG), "ab"[32 * b >= TC[t][1]]
             d = T[sg][:, 64 * b:64 * b + 64]
-            tt(d, d, T.TR[:], A.is_gt, [sg + "_0", sg + "_1", "TR"], [sg + "d"])
+            tt(d, d, T.TR[:], A.is_gt, [sg + "_0" + s, sg + "_1" + s, "TR"], [sg + "d"])
 
         def weigh(b, side):
-            sg, half, gn, e = "SG%d" % (b % NSG), str(2 * b // NB), "G%d" % (b // 2 % NG), 32 * b + 32
+            sg, gn, e, cut = "SG%d" % (b % NSG), "G%d" % (b // 2 % NG), 32 * b + 32, TC[t][1]
+            reach = "ab" if (side == "r") == (e <= cut) else "b" if side == "r" else "a"
             for h in range(2):
-                k, c = 2 * (b % 2) + h, 3 * (2 * b + h) + 2
-                w, names = T.Q3[:, c:c + 1], ([sg + "_%d" % h, "Q3" + half], [gn + "_%d%s" % (k, side)])
+                k, c = 2 * (b % 2) + h, 4 * (2 * b + h) + 3
+                w = T.Q4[:, c:c + 1]
+                names = ([sg + "_%d%s" % (h, s) for s in reach] + ["Q4%d" % (e > cut)], [gn + "_%d%s" % (k, side)])
+                end = DIRECT.get(b, C)
+                if side == "d":
+                    bank = ps((P, Q)[h][3])
+                    ts("v", T[gn][:, 4 * end + k:4 * C:4], T[bank][:, end:C], T.ST[:, 4 * c - 12:4 * c - 11], w,
+                       A.is_le if buys else A.is_ge, A.mult, [bank, "ST%d" % (e > cut), names[0][-1]], names[1])
+                    continue
                 if side == "r":
-                    if e < C:
-                        ts("v", T[gn][:, 4 * e + k:4 * C:4], T[sg][:, 2 * e + h:2 * C:2], 0.0, w, A.is_ge, A.mult, *names)
+                    if e < end:
+                        ts("v", T[gn][:, 4 * e + k:4 * end:4], T[sg][:, 2 * e + h:2 * end:2], 0.0, w, A.is_ge, A.mult, *names)
                     continue
                 names[0].append(sg + "d")
                 if b in SCALAR_LEFT:
-                    op("s", lambda E: E.activation(T[gn][:, k:4 * e:4], T[sg][:, h:2 * e:2], AF.Relu, scale=w), *names)
+                    part = int(e > cut)
+                    if part not in widened:
+                        a0, a1 = runs(TC[t])[part]
+                        cp("s", T.QS[:, a0 // 16:a1 // 16], T.Q4[:, a0 // 4 + 3:a1 // 4:4], ["Q4%d" % part], ["QS%d" % part])
+                        widened.append(part)
+                    act(T[gn][:, k:4 * e:4], T[sg][:, h:2 * e:2], AF.Relu, names[0] + ["QS%d" % part], names[1],
+                        scale=T.QS[:, c // 4:c // 4 + 1])
                 else:
                     ts("v", T[gn][:, k:4 * e:4], T[sg][:, h:2 * e:2], 0.0, w, A.is_gt, A.mult, *names)
 
@@ -304,11 +350,13 @@ def rank_program(g, core, T, topo):
         ready = [0] * (NB // 2)
         for b in range(NB):
             ready[b // 2] = max(ready[b // 2], b + 1 + (DELAY if b in SCALAR_LEFT else 0))
-        packed = 0
-        signs(0)
+        packed, widened = 0, []
+        signs(t, 0, "b" if EARLY[t] else "ab")
         for b in range(NB):
+            if b in DIRECT:
+                weigh(b, "d")
             if b + 1 < NB:
-                signs(b + 1)
+                signs(t, b + 1, "b" if b + 1 < EARLY[t] else "ab")
             if b - DELAY in SCALAR_LEFT:
                 weigh(b - DELAY, "l")
             if not (b == last and last in SCALAR_LEFT):
@@ -323,108 +371,107 @@ def rank_program(g, core, T, topo):
             if b not in SCALAR_LEFT:
                 weigh(b, "l")
             if b == 0:
-                turn(1, not buys)
-                if t > 0:
-                    for c in range(4):
-                        mm(4 + c, "EQ", "ES", 128 * c, TQ, TS, True, True, ["EQ_0"] + both(TQ))
+                turn(t, 1, not buys)
+            if t > 0 and b == max([0] + list(DIRECT)):
+                unpack(P[2:] + Q[2:], TQ, TS, whole, True, True)
         pack(NB // 2 - 1)
-        if t == 0:
-            for b in range(4):
-                op("s", lambda E: E.activation(T.EB[:, 512 * b + b:512 * b + 512:4], T.IA[:], AF.Relu, bias=1.0, scale=-1.0),
-                   ["IA"], ["EB_%d" % b])
-        for k in range(2):
-            a, ex = H * k, "EXh%d" % k
-            wrap("EX", T["ps%d" % (3 - k)][:, 0:H], ["ps%d" % (3 - k)], [ex], a, a + H)
-            ts("v", part(SO, k), T.EX[:, a + 15:a + H:16], T.XO[:, 0:1], None, A.add, None, [ex, "XO0"], [SO + "h%d" % k])
-            send(dst, "rS%d%d" % (t, k), [(part(SP, k), part(SO, k), [SO + "h%d" % k], [SP + "h%d" % k])])
-        ts("v", T.NO[:], T.EX[:, 15:C:16], T.XO[:, 0:1], 1.0, A.add, A.add, halves("EX") + ["XO0"], ["NO"])
+        for k, (a, b) in enumerate(runs(UC)):
+            c, d = a // 16, b // 16
+            wrap("EX", T[ps(P[k])][:, 0:b - a], [ps(P[k])], ["EX_%d" % a], a, b, "XP")
+            ts("v", T[SO][:, c:d], T.EX[:, a + 15:b:16], T.XO[:, 2:3], None, A.add, None, ["EX_%d" % a, "XO"], [SO + "_%d" % a])
+            send(dst, "rS%d%d" % (t, k), [(T[SP][:, c:d], T[SO][:, c:d], [SO + "_%d" % a], [SP + "_%d" % a])])
 
-        def mark(name, k):
-            cp("v", T[MK][:].indirect(part(name, k)), T.ONE[:], [name + "h%d" % k, "ONE"], [MK])
+        def mark(name, a, b):
+            cp("v", T[MK][:].indirect(T[name][:, a // 16:b // 16]), T.ONE[:, a:b],
+               [name + "_%d" % c for c in UC[:-1] if a <= c < b] + ["ONE"], [MK])
 
-        mark(SO, 0)
+        ts("v", T.GO[:], T.EX[:, 15:C:16], T.XO[:, 3:4], 0.5, A.add, A.mult, parts("EX", UC) + ["XO"], ["GO"])
+        mark(SO, 0, C)
         if t == 0:
-            quant("EQ", "ES", 0, 512, "EB", slots("EB"))
+            ts("v", T.XF[:], T.XD[:], -2 * BIG, -AGE, A.mult, A.add, ["XD"], ["XF"])
             for b in range(4):
-                mm(4 + b, "EQ", "ES", 128 * b, TQ, TS, True, True, ["EQ_0"] + both(TQ))
-        ts("v", T.HO[:], T.NO[:], 1, None, A.logical_shift_right, None, ["NO"], ["HO"])
-        ts("v", T.EO[:], T.NO[:], 1, None, A.bitwise_and, None, ["NO"], ["EO"])
-        mark(SO, 1)
-        cp("v", T.GO[:], T.HO[:], ["HO"], ["GO"])
-        mark(SP, 0)
-        tt(T.XE[:, 15:C:16], T.XP[:, 15:C:16], T.EO[:], A.add, ["XP", "EO"], ["XE"])
-        for b in range(4):
-            cp("s", T.DO[:, C * b:C * b + C], T["ps%d" % (4 + b)][:, 0:C], ["ps%d" % (4 + b)], ["DO_%d" % b], 0.5)
-        for b in range(4):
-            mm(b, "EQ", "ES", 128 * b, LQ, LS, True, True, ["EQ_0", LQ, LS])
-        for b in range(4):
-            mm(4 + b, "EQ", "ES", 128 * b, TQ, TS, True, False, ["EQ_0"] + both(TQ), 0, H)
-        mark(SP, 1)
-        scan(T.SEG[:, 1:UN // 2 + 1], T[MK][:, 0:UN:2], T[MK][:, 1:UN:2], 0.0, A.add, A.add, [MK], ["SEG"])
-        for k in range(2):
-            cp("vs"[k], T.FR[:, H * k:H * k + H], T.SEG[:, 0:UN // 2 + 1].indirect(T.GO[:, KH * k:KH * k + KH]),
-               ["SEG", "GO"], ["FRh%d" % k])
-        for b in range(4):
-            cp("s", T.DP[:, C * b:C * b + C], T["ps%d" % b][:, 0:C], ["ps%d" % b], ["DP_%d" % b], 0.5)
-        wrap("EY", T.FR[:], halves("FR"), ["EY"], pattern="XE")
-        ts("v", T.FS[:], T.EY[:, 15:C:16], T.XO[:, 1:2], None, A.add, None, ["EY", "XO1"], ["FS"])
+                quant("EQ", "ES", 128 * b, 128 * b + 128, T.EB[:, 3 - b:515 - b], ["EB"], ["EQ_%d" % b])
+            tt(T.XG[:], T.XF[:], T.XA[:], A.add, ["XA", "XF"], ["XG"])
+            unpack(P[2:] + Q[2:], TQ, TS, whole, True, True)
+        ts("v", T.EO[:], T.GO[:], -2.0, T.XO[:, 5:6], A.mult, A.add, ["GO", "XO5"], ["EO"])
+        tt(T.XE[:, 15:C:16], T.EX[:, 15:C:16], T.EO[:], A.add, parts("EX", UC) + ["EO"], ["XE"])
+        mark(SP, *runs(UC)[0])
+        unpack(Q[:2] + P[:2], LQ, LS, [LQ, LS], True, True)
+        halves = [("DO", b, bank) for b, bank in enumerate(P[2:] + Q[2:])] + [("DP", b, bank) for b, bank in enumerate(Q[:2] + P[:2])]
+        for i, (name, b, bank) in enumerate(halves):
+            if i == BEFORE[t]:
+                for a, c in runs(UC)[1:]:
+                    mark(SP, a, c)
+                scan(T.SEG[:, 1:UN // 2 + 1], T[MK][:, 0:UN:2], T[MK][:, 1:UN:2], 0.0, A.add, A.add, [MK], ["SEG"])
+                for k in range(2):
+                    cp("vs"[k], T.FR[:, C // 2 * k:C // 2 * (k + 1)],
+                       T.SEG[:, 0:UN // 2 + 1].indirect(T.GO[:, K // 2 * k:K // 2 * (k + 1)]), ["SEG", "GO"], ["FR%d" % k])
+                if t == 0:
+                    cp("s", T.XH[:], T.XG[:].indirect(T.RO[:]), ["XG", "RO"], ["XH"])
+            act(T[name][:, C * b:C * b + C], T[ps(bank)][:, 0:C], AF.Copy, [ps(bank)], [name + "_%d" % b], scale=0.5)
+        unpack(P, TQ, TS, whole, True, False, *runs(TC[t + 1])[0])
+        wrap("EY", T.FR[:], ["FR0", "FR1"], ["EY"], 0, C, "XE")
+        ts("v", T.FS[:], T.EY[:, 15:C:16], T.XO[:, 0:1], None, A.add, None, ["EY", "XO"], ["FS"])
         cp("v", T[AO][:].indirect(T.FS[:]), T.IO[:, 0:C], ["FS", "IO"], [AO])
-        for k in range(2):
-            a, c, hk = H * k, KH * k, "h%d" % k
-            scan(T.FI[:, a:a + H], T[AO][:, a:a + H], T.M512[:], T.FI[:, a - 1:a] if k else float(LOW), A.max, A.add,
-                 [AO, "M512"] + ["FIh0"] * k, ["FI" + hk])
-            wrap("EX", T.FI[:, a:a + H], ["FI" + hk], ["EX" + hk], a, a + H)
-            ts("v", T.LI[:, c:c + KH], T.EX[:, a + 15:a + H:16], T.XO[:, 2:3], None, A.add, None, ["EX" + hk, "XO2"], ["LI" + hk])
-            ts("v", T.LJ[:, c:c + KH], T.LI[:, c:c + KH], 511, None, A.bitwise_and, None, ["LI" + hk], ["LJ" + hk])
-            cp("v", part(LO, k), T.LJ[:, c:c + KH], ["LJ" + hk], [LO + hk])
-            send(dst, "rL%d%d" % (t, k), [(part(LP, k), part(LO, k), [LO + hk], [LP + hk])])
-        ts("v", T.FO[:], T.EY[:, 15:C:16], T.XO[:, 1:2], float(C), A.add, A.min, ["EY", "XO1"], ["FO"])
-        for k in range(2):
-            for b in range(4):
-                cp("v" if k == 1 and b < 2 else "s", T.ZT[:, C * b + H * k:C * b + H * k + H],
-                   T.DO[:, C * b:C * b + C].indirect(part(LO, k)), ["DO_%d" % b, LO + "h%d" % k], ["ZT_%d%d" % (b, k)])
+        for k, (a, b) in enumerate(runs(ZC)):
+            c, d, e = a // 16, b // 16, "_%d" % a
+            wrap("EZ", T[AO][:, a:b], [AO] + ["EZ_%d" % ZC[k - 1]] * (k > 0), ["EZ" + e], a, b, "XH",
+                 T.EZ[:, a - 1:a] if k else float(LOW))
+            tt(T.LI[:, c:d], T.EZ[:, a + 7:b:16], T.EZ[:, a + 15:b:16], A.max, ["EZ" + e], ["LI" + e])
+            ts("v", T.LJ[:, c:d], T.LI[:, c:d], int(AGE) - 1, None, A.bitwise_and, None, ["LI" + e], ["LJ" + e])
+            cp("v", T[LO][:, c:d], T.LJ[:, c:d], ["LJ" + e], [LO + e])
+            send(dst, "rL%d%d" % (t, k), [(T[LP][:, c:d], T[LO][:, c:d], [LO + e], [LP + e])])
+        ts("v", T.FO[:], T.EY[:, 15:C:16], T.XO[:, 0:1], float(C), A.add, A.min, ["EY", "XO"], ["FO"])
         if t == 1:
-            quant("VQ", "VS", 0, 128, "VB", ["VB"])
-            cp("s", T.OL[:], T.IO[:].indirect(T.FO[:]), ["IO", "IOz", "FO"], ["OL"])
-            dma("y", "dol", [(T.ol[:], T.OL[0:128:16, :], ["OL"], [])])
+            quant("VQ", "VS", 0, 128, T.VB[:], ["VB"], ["VQ"])
 
-        for k in range(2):
-            a = H * k
-            for b in range(4):
-                tt(T.Z[:, 4 * a + b:4 * (a + H):4], T.DP[:, C * b:C * b + C].indirect(part(LP, k)),
-                   T.ZT[:, C * b + a:C * b + a + H], A.add, ["DP_%d" % b, LP + "h%d" % k, "ZT_%d%d" % (b, k)],
-                   ["Z_%d%d" % (b, k)])
-            quant("ZQ", "ZS", a, a + H, "Z", slots("Z", k))
-            for b in range(4):
-                mm(b, "WQ", "WS", 128 * b, "ZQ", "ZS", True, True, ["WQ", "WS", "ZQ_%d" % a], a, a + H)
-            for b in range(4):
-                bank = "ps%d" % b
-                out, src, names = T.HP[:, HW * b + a:HW * b + a + H], T[bank][:, 0:H], ([bank], ["HP_%d%d" % (b, k)])
-                if k == 1 and b % 2 == 0:
+        def own_parts(k):
+            a, b = runs(ZC)[k]
+            for i in range(4):
+                cp(OWN_ON[k][i], T.ZT[:, C * i + a:C * i + b], T.DO[:, C * i:C * i + C].indirect(T[LO][:, a // 16:b // 16]),
+                   ["DO_%d" % i, LO + "_%d" % a], ["ZT_%d%d" % (i, k)])
+
+        def relu(k):
+            a, b = runs(ZC)[k]
+            for i, bank in enumerate(Q):
+                out, src, names = T.HP[:, HW * i + a:HW * i + b], T[ps(bank)][:, 0:b - a], ([ps(bank)], ["HP_%d%d" % (i, k)])
+                if RELU_ON[k][i] == "v":
                     ts("v", out, src, 0.0, 0.03125, A.max, A.mult, *names)
                 else:
-                    op("s", lambda E: E.activation(out, src, AF.Relu, scale=0.03125), *names)
-        for b in range(4):
-            mm(b, "EQ", "ES", 128 * b, TQ, TS, True, False, ["EQ_0"] + both(TQ), H, C)
-        for k in range(2):
-            a, o = H * k, KH * k
-            for b in range(4):
-                cp("vs"[b % 2], T.HT[:, 4 * a + b:4 * (a + H):4], T.HP[:, HW * b:HW * b + HW].indirect(T.FO[:, o:o + KH]),
-                   ["HP_%d0" % b, "HP_%d1" % b, "HPz%d" % b, "FO"], ["HT_%d%d" % (b, k)])
-            quant("HQ", "HS", a, a + H, "HT", slots("HT", k))
-            for b in range(4):
-                mm(4 - 4 * k + b, "EQ", "ES", 128 * b, "HQ", "HS", False, True, ["EQ_0", "HQ_%d" % a], a, a + H)
-        for k in range(2):
-            a = H * k
-            for b in range(4):
-                bank = "ps%d" % (4 - 4 * k + b)
-                cp("ssss"[b] if k == 0 else "svsv"[b], T[XN][:, 4 * a + b:4 * (a + H):4], T[bank][:, 0:H],
-                   [bank], [XN + "_%d%d" % (b, k)])
-            quant(NQ, NS, a, a + H, XN, slots(XN, k))
+                    act(out, src, AF.Relu, *names, scale=0.03125)
+
+        for k in range(len(ZC) - 1):
+            own_parts(k)
+        for k, (a, b) in enumerate(runs(ZC)):
+            for i in range(4):
+                tt(T.Z[:, 4 * a + i:4 * b:4], T.DP[:, C * i:C * i + C].indirect(T[LP][:, a // 16:b // 16]),
+                   T.ZT[:, C * i + a:C * i + b], A.add, ["DP_%d" % i, LP + "_%d" % a, "ZT_%d%d" % (i, k)], ["Z_%d%d" % (i, k)])
+            quant("ZQ", "ZS", a, b, T.Z[:, 4 * a:4 * b], slots("Z", k), ["ZQ_%d" % a])
+            for i, bank in enumerate(Q):
+                mm(bank, "WQ", "WS", 128 * i, "ZQ", "ZS", True, True, ["WQ", "WS", "ZQ_%d" % a], a, b)
+            relu(k)
+            if t == 1 and k == 0:
+                cp("s", T.OL[:], T.IO[:].indirect(T.FO[:]), ["IO", "IOz", "FO"], ["OL"])
+                dma("y", "dol", [(T.ol[:], T.OL[0:128:16, :], ["OL"], [])])
+        unpack(Q, TQ, TS, whole, True, False, *runs(TC[t + 1])[1])
+        for k, (a, b) in enumerate(runs(TC[t + 1])):
+            for i in range(4):
+                cp(PICK_ON[k][i], T.HT[:, 4 * a + i:4 * b:4], T.HP[:, HW * i:HW * i + HW].indirect(T.FO[:, a // 16:b // 16]),
+                   ["HP_%d%d" % (i, j) for j in range(len(ZC) - 1)] + ["HPz%d" % i, "FO"], ["HT_%d%d" % (i, k)])
+            quant("HQ", "HS", a, b, T.HT[:, 4 * a:4 * b], slots("HT", k), ["HQ_%d" % a])
+            unpack((P, Q)[k], "HQ", "HS", ["HQ_%d" % a], False, True, a, b)
+        for k, (a, b) in enumerate(runs(TC[t + 1])):
+            for i, bank in enumerate((P, Q)[k]):
+                cp(STATE_ON[k][i], T[XN][:, 4 * a + i:4 * b:4], T[ps(bank)][:, 0:b - a], [ps(bank)], [XN + "_%d%d" % (i, k)])
+            state(t + 1, k)
             if t == 1:
-                mm(4 + k, "VQ", "VS", 0, NQ, NS, True, True, ["VQ_0", NQ + "_%d" % a], a, a + H)
+                mm((P, Q)[k][0], "VQ", "VS", 0, NQ, NS, True, True, ["VQ", NQ + "_%d" % a], a, b)
             elif k == 0:
-                scores(t + 1, 0)
+                scores(1, 0)
+            else:
+                turn(1, 0, rank > rank ^ STEP[1])
+                for b in range(EARLY[1]):
+                    signs(1, b, "a")
 
     def store(e, out, in_, rd):
         order(e, rd, [], False)
@@ -432,15 +479,17 @@ def rank_program(g, core, T, topo):
         total["dst"] += 16
 
     def codes(k):
-        store("y", T.oc[:, 4 * H * k:4 * H * (k + 1)], T.TQ2[:, H * k:H * (k + 1)].bitcast(dt.uint8), ["TQ2_%d" % (H * k)])
+        a, b = runs(TC[2])[k]
+        store("y", T.oc[:, 4 * a:4 * b], T.TQ2[:, a:b].bitcast(dt.uint8), ["TQ2_%d" % a])
 
     def scales(e, k):
-        store(e, T.osc[4 * k:4 * k + 4, :], T.TS2[32 * k:32 * k + 4, :], both("TQ2"))
+        store(e, T.osc[4 * k:4 * k + 4, :], T.TS2[32 * k:32 * k + 4, :], parts("TQ2", TC[2]))
 
     def result(k):
-        a, bank = H * k, "ps%d" % (4 + k)
-        cp("sv"[k], T.YS[:, a:a + H], T[bank][:, 0:H], [bank], ["YS%d" % k])
-        store("s", T.y[:, a:a + H], T.YS[:, a:a + H], ["YS%d" % k])
+        a, b = runs(TC[2])[k]
+        bank = ps((P, Q)[k][0])
+        cp("sv"[k], T.YS[:, a:b], T[bank][:, 0:b - a], [bank], ["YS%d" % k])
+        store("s", T.y[:, a:b], T.YS[:, a:b], ["YS%d" % k])
 
     codes(0)
     result(0)

@@ -11,17 +11,21 @@ AGE = 512.0
 STEP = [1, 2]
 TC = [[0, 224, C], [0, 224, C], [0, 224, C]]
 UC = [0, 160, C]
-ZC = [0, 224, C]
-EARLY = [0, 0]
-SCALAR_LEFT = [0, 1, 13]
-DIRECT = {}
+LC = [0, 160, C]
+ZC = [0, 160, 320, C]
+EARLY = [3, 4]
+AHEAD = [2, 3]
+FIRST = 0
+DIRECT = [[0, 1], [0, 1]]
+SCALAR_LEFT = [13]
 DELAY = 2
+OPENING = ["x0", "x1", "s0", "e0", "e1", "x2", "x3"]
+SECOND = ["f0", "g0", "f1", "g1", "s1"]
 BEFORE = [2, 5]
-OWN_ON = ["ssss", "vvss"]
-RELU_ON = ["ssss", "vsvs"]
-PICK_ON = ["vsvs", "vsvs"]
-STATE_ON = ["ssss", "svsv"]
-NSG, NG = 6, 4
+OWN_ON = ["ssss", "ssss"]
+PICK_ON = ["svsv", "svsv"]
+SHARE = False
+TURN = 1
 P, Q = [0, 1, 2, 3], [4, 5, 6, 7]
 
 F32, BF, I32, U16, CODE, U8 = "float32", "bfloat16", "int32", "uint16", "float8_e4m3fn_x4", "uint8"
@@ -44,20 +48,17 @@ for _n, _w, _d in [
         ("LO0", 32, U16), ("LO1", 32, U16), ("LP0", 32, U16), ("LP1", 32, U16),
         ("FO", K, U16), ("FS", K, U16), ("LI", K, I32), ("LJ", K, I32), ("EO", K, F32), ("GO", K, U16),
         ("MK0", UN, BF), ("MK1", UN, BF), ("SEG", UN // 2 + 16, F32), ("AO0", 2 * C, F32), ("AO1", 2 * C, F32),
-        ("DO", 4 * C, BF), ("DP", 4 * C, BF), ("ZT", 4 * C, BF), ("Z", 4 * C, BF), ("ZQ", C, CODE), ("ZS", C, U8),
+        ("DO", 4 * C, BF), ("DP", 4 * C, BF), ("DT", 4 * C, BF), ("ZT", 4 * C, BF), ("Z", 4 * C, BF),
+        ("ZQ", C, CODE), ("ZS", C, U8),
         ("HP", 4 * HW, BF), ("HT", 4 * C, BF), ("HQ", C, CODE), ("HS", C, U8), ("YS", C, F32), ("OL", C, F32)]:
     SCRATCH[_n] = ("sbuf", [128, _w], _d)
-for _i in range(NSG):
-    SCRATCH["SG%d" % _i] = ("sbuf", [128, 2 * C], BF)
-for _i in range(NG):
-    SCRATCH["G%d" % _i] = ("sbuf", [128, 4 * C], BF)
-    SCRATCH["GQ%d" % _i] = ("sbuf", [128, C], CODE)
-    SCRATCH["GS%d" % _i] = ("sbuf", [128, C], U8)
+for _n, _w, _d in [("SG", 2 * C * NB, BF), ("G", 2 * C * NB, BF), ("GQ", C * NB // 2, CODE), ("GS", C * NB // 2, U8)]:
+    SCRATCH[_n] = ("sbuf", [128, _w], _d)
 for _i in range(8):
     SCRATCH["ps%d" % _i] = ("psum", [128, 512], F32)
 SEMAPHORES = (["cv", "cs", "ct", "cg", "dx0", "dx1", "du", "dv", "dw", "dol", "sent", "rT0", "rT1", "dst"]
               + ["rS%d%d" % (_t, _k) for _t in range(2) for _k in range(len(UC) - 1)]
-              + ["rL%d%d" % (_t, _k) for _t in range(2) for _k in range(len(ZC) - 1)])
+              + ["rL%d%d" % (_t, _k) for _t in range(2) for _k in range(len(LC) - 1)])
 
 A = AluOpType
 AF = ActivationFunctionType
@@ -140,11 +141,11 @@ def rank_program(g, core, T, topo):
             for k in land:
                 writer[k] = [(sem, total[sem])]
 
-    def ts(e, out, in0, s1, s2, o0, o1, rd, wr):
+    def ts(out, in0, s1, s2, o0, o1, rd, wr):
         if s2 is None:
-            op(e, lambda E: E.tensor_scalar(out, in0, s1, None, o0), rd, wr)
+            op("v", lambda E: E.tensor_scalar(out, in0, s1, None, o0), rd, wr)
         else:
-            op(e, lambda E: E.tensor_scalar(out, in0, s1, s2, o0, o1), rd, wr)
+            op("v", lambda E: E.tensor_scalar(out, in0, s1, s2, o0, o1), rd, wr)
 
     def tt(out, a, b, o, rd, wr):
         op("v", lambda E: E.tensor_tensor(out, a, b, o), rd, wr)
@@ -170,10 +171,12 @@ def rank_program(g, core, T, topo):
     def quant(qn, sn, a, b, src, rd, wr):
         op("v", lambda E: E.quantize_mx(T[qn][:, a:b], T[sn][:, a:b], src), rd, wr)
 
+    def ps(bank):
+        return "ps%d" % bank
+
     def mm(bank, wq, ws, wa, xq, xs, start, stop, rd, a=0, b=C):
-        bank = "ps%d" % bank
-        op("t", lambda E: E.matmul_mx(T[bank][:, 0:b - a], T[wq][:, wa:wa + 128], T[ws][:, wa:wa + 128],
-                                      T[xq][:, a:b], T[xs][:, a:b], start, stop), rd, [bank], acc=not start)
+        op("t", lambda E: E.matmul_mx(T[ps(bank)][:, 0:b - a], T[wq][:, wa:wa + 128], T[ws][:, wa:wa + 128],
+                                      T[xq][:, a:b], T[xs][:, a:b], start, stop), rd, [ps(bank)], acc=not start)
 
     def scan(out, d0, d1, init, o0, o1, rd, wr):
         op("v", lambda E: E.tensor_tensor_scan(out, d0, d1, init, o0, o1), rd, wr)
@@ -184,36 +187,101 @@ def rank_program(g, core, T, topo):
     def slots(n, k=""):
         return [n + "_%d%s" % (b, k) for b in range(4)]
 
-    def parts(n, edges):
-        return [n + "_%d" % a for a in edges[:-1]]
+    def parts(n, edges, a=0, b=C):
+        return [n + "_%d" % c for c, d in runs(edges) if c < b and d > a]
 
-    def ps(bank):
-        return "ps%d" % bank
-
-    def unpack(banks, qn, sn, rd, start, stop, a=0, b=C):
-        for i in range(4):
+    def unpack(banks, qn, sn, rd, start, stop, a=0, b=C, planes=range(4)):
+        for i in planes:
             mm(banks[i], "EQ", "ES", 128 * i, qn, sn, start, stop, ["EQ_%d" % i] + rd, a, b)
 
-    def scores(t, k):
-        a, b = runs(TC[t])[k]
-        tq, tsc, banks = "TQ%d" % t, "TS%d" % t, (P, Q)[k]
-        rd = ["UP", "UPS"] + parts(tq, TC[t][:k + 2])
-        todo = [(banks[h], 128 * h, 0) for h in range(2) if k or EARLY[t]]
-        todo.insert(2 * k, (banks[2], 256, a))
-        if k and DIRECT:
-            todo += [((P, Q)[h][3], 128 * h, 0) for h in range(2)]
-        for bank, wa, a0 in todo:
-            mm(bank, "UP", "UPS", wa, tq, tsc, True, True, rd, a0, b)
+    def buyer(t):
+        return rank < rank ^ STEP[t]
 
-    def turn(t, k, negate):
+    def state(t, k):
         a, b = runs(TC[t])[k]
-        bank = ps((P, Q)[k][2])
+        quant("TQ%d" % t, "TS%d" % t, a, b, T["X%d" % t][:, 4 * a:4 * b], slots("X%d" % t, k), ["TQ%d_%d" % (t, a)])
+
+    def product(t, name):
+        kind, i, cut = name[0], int(name[1]), TC[t][1]
+        bank, wa = (P[2 + i], 256) if kind == "s" else ({"e": P, "g": Q, "f": Q[2:]}[kind][i], 128 * i)
+        a, b = (0, C) if kind == "f" else (cut, C) if name in ("s1", "g0", "g1") else (0, cut)
+        if kind in "sf" or EARLY[t]:
+            mm(bank, "UP", "UPS", wa, "TQ%d" % t, "TS%d" % t, True, True, ["UP", "UPS"] + parts("TQ%d" % t, TC[t], a, b), a, b)
+
+    def turn(t, k):
+        a, b = runs(TC[t])[k]
+        bank = ps(P[2 + k])
         op("v", lambda E: E.transpose(T.ST[:, a:b], T[bank][:, 0:b - a]), [bank], ["ST%d" % k])
-        if negate:
-            act(T.PN[:, a // 16:b // 16], T.ST[:, a:b:16], AF.Copy, ["ST%d" % k], ["PN%d" % k], scale=-1.0)
-        ts("v", T.QF[:, a // 4:b // 4], T.ST[:, a:b:4], 0.0, None, A.is_gt, None, ["ST%d" % k], ["QF%d" % k])
+        if not buyer(t):
+            ts(T.PN[:, a // 16:b // 16], T.ST[:, a:b:16], -1.0, None, A.mult, None, ["ST%d" % k], ["PN%d" % k])
+        ts(T.QF[:, a // 4:b // 4], T.ST[:, a:b:4], 0.0, None, A.is_gt, None, ["ST%d" % k], ["QF%d" % k])
         scan(T.Q4[:, a // 4:b // 4], T.QP[:, a // 4:b // 4], T.QF[:, a // 4:b // 4], 1.0, A.min, A.add,
              ["QP", "QF%d" % k], ["Q4%d" % k])
+
+    def sign(t, b, h, side):
+        sg, cut, c, s0 = "SG%d" % b, TC[t][1], 2 * b + h, 2 * C * b
+        a0, a1 = cut if side == "b" else 0, cut if side == "a" else C
+        bank = ps({"a": P, "b": Q if SHARE else Q[2:], "ab": Q[2:]}[side][h])
+        o = cut if side == "b" and SHARE else 0
+        p, pn = (T.ST[:, 16 * c:16 * c + 1], "ST") if buyer(t) else (T.PN[:, c:c + 1], "PN")
+        act(T.SG[:, s0 + 2 * a0 + h:s0 + 2 * a1:2], T[bank][:, a0 - o:a1 - o], AF.Sign, [bank, pn + str(int(32 * b >= cut))],
+            [sg + "_%d%s" % (h, s) for s in side] + [sg + "d"] * ((1 - h) * ("a" in side)),
+            bias=p, scale=-1.0 if buyer(t) else 1.0)
+
+    def ties(t, b):
+        sg, s = "SG%d" % b, "ab"[32 * b >= TC[t][1]]
+        d = T.SG[:, (2 * C + 64) * b:(2 * C + 64) * b + 64]
+        tt(d, d, T.TR[:], A.is_gt, [sg + "_0" + s, sg + "_1" + s, "TR"], [sg + "d"])
+
+    def weigh(t, b, side):
+        sg, gn, e, cut = "SG%d" % b, "G%d" % (b // 2), 32 * b + 32, TC[t][1]
+        s0, g0 = 2 * C * b, 4 * C * (b // 2)
+        part, end = int(e > cut), cut if b in DIRECT[t] or b < AHEAD[t] else C
+        if side == "e":
+            side, e, end = "r", cut, C
+        reach = "ab" if (side == "l" and part) or (side == "r" and e < cut < end) else "b" if e >= cut and side == "r" else "a"
+        for h in range(2):
+            k, c = 2 * (b % 2) + h, 2 * b + h
+            w, wr = T.Q4[:, 4 * c + 3:4 * c + 4], [gn + "_%d%s" % (k, "d" if e == cut != 32 * b + 32 else side)]
+            rd = [sg + "_%d%s" % (h, s) for s in reach] + ["Q4%d" % part]
+            if side == "d":
+                ts(T.G[:, g0 + 4 * cut + k:g0 + 4 * C:4], T[ps(Q[h])][:, 0:C - cut], T.ST[:, 16 * c:16 * c + 1],
+                   T.QS[:, c:c + 1], A.is_le if buyer(t) else A.is_ge, A.mult, [ps(Q[h]), "ST0", "QSd"], wr)
+            elif side == "r":
+                if e < end:
+                    ts(T.G[:, g0 + 4 * e + k:g0 + 4 * end:4], T.SG[:, s0 + 2 * e + h:s0 + 2 * end:2], 0.0, w,
+                       A.is_ge, A.mult, rd, wr)
+            else:
+                out, src = T.G[:, g0 + k:g0 + 4 * e:4], T.SG[:, s0 + h:s0 + 2 * e:2]
+                if b not in SCALAR_LEFT:
+                    ts(out, src, 0.0, w, A.is_gt, A.mult, rd + [sg + "d"], wr)
+                    continue
+                if h == 0:
+                    cp("s", T.QS[:, c:c + 2], T.Q4[:, 4 * c + 3:4 * c + 8:4], ["Q4%d" % part], ["QS%d" % b])
+                act(out, src, AF.Relu, rd + [sg + "d", "QS%d" % b], wr, scale=T.QS[:, c:c + 1])
+
+    def pack(i):
+        gq, o, last = "GQ%d" % i, C * i, i == NB // 2 - 1
+        rd = [k for side in "lrd" for k in slots("G%d" % i, side)]
+        if not last:
+            quant("GQ", "GS", o, o + C, T.G[:, 4 * o:4 * (o + C)], rd, parts(gq, UC))
+        for k, (a, b) in enumerate(runs(UC)):
+            if last:
+                quant("GQ", "GS", o + a, o + b, T.G[:, 4 * (o + a):4 * (o + b)], rd, [gq + "_%d" % a])
+            mm(P[k], "CQ", "CS", 0, "GQ", "GS", i == 0, last, ["CQ", gq + "_%d" % a], o + a, o + b)
+
+    def early(t):
+        first = min(EARLY[t], 2)
+        for b, h in [(b, h) for h in range(2) for b in range(first)] + [(b, h) for b in range(first, EARLY[t]) for h in range(2)]:
+            sign(t, b, h, "a")
+            if (b, h) == (first - 1, 0) and DIRECT[t]:
+                n = 2 * max(DIRECT[t]) + 2
+                cp("s", T.QS[:, 0:n], T.Q4[:, 3:4 * n:4], ["Q40"], ["QSd"])
+
+    def ahead(t, b):
+        ties(t, b)
+        weigh(t, b, "r")
+        weigh(t, b, "l")
 
     dma("s", "du", [(T.UB[:], T.u[:], [], ["UB"])])
     for k, (a, b) in enumerate(runs(TC[0])):
@@ -228,65 +296,52 @@ def rank_program(g, core, T, topo):
     iota("I2", T.I2[:], [[1, 8], [0, 32], [-1, 2]], 0, 0)
     fill(T.QP[:], 1000.0, ["QP"])
     fill(T.QP[:, 1:C // 4:4], 1.0, ["QP"])
-    ts("v", T.PJ[:, 0:2], T.PI[:], 15, None, A.bitwise_and, None, ["PI"], ["PJ0"])
-    ts("v", T.PJ[:, 2:3], T.PI[:, 0:1], 31, None, A.bitwise_and, None, ["PI"], ["PJ2"])
-    ts("v", T.PJ[:, 3:4], T.PI[:, 0:1], 4, 6, A.logical_shift_right, A.bitwise_and, ["PI"], ["PJ3"])
-    ts("v", T.PJ[:, 4:5], T.PI[:, 0:1], 2, 3, A.logical_shift_right, A.bitwise_and, ["PI"], ["PJ4"])
-    ts("v", T.PJ[:, 5:6], T.PI[:, 0:1], 8, None, A.bitwise_and, None, ["PI"], ["PJ5"])
+    ts(T.PJ[:, 0:2], T.PI[:], 15, None, A.bitwise_and, None, ["PI"], ["PJ0"])
+    ts(T.PJ[:, 2:3], T.PI[:, 0:1], 31, None, A.bitwise_and, None, ["PI"], ["PJ2"])
+    ts(T.PJ[:, 3:4], T.PI[:, 0:1], 4, 6, A.logical_shift_right, A.bitwise_and, ["PI"], ["PJ3"])
+    ts(T.PJ[:, 4:5], T.PI[:, 0:1], 2, 3, A.logical_shift_right, A.bitwise_and, ["PI"], ["PJ4"])
+    ts(T.PJ[:, 5:6], T.PI[:, 0:1], 8, None, A.bitwise_and, None, ["PI"], ["PJ5"])
     cp("v", T.UO[:, 0:16], T.UI[:, 0:16], ["UI"], ["UO0"])
     cp("v", T.PF[:], T.PJ[:], ["PJ0", "PJ2", "PJ3", "PJ4", "PJ5"], ["PF"])
-    ts("v", T.UO[:, 16:24], T.K16[:, 0:8], 16.0, T.PF[:, 4:5], A.mult, A.add, ["K16", "PF"], ["UO1"])
-    ts("v", T.XA[:], T.K16[:], T.PF[:, 0:1], BIG, A.is_equal, A.mult, ["K16", "PF"], ["XA"])
-    ts("v", T.XB[:], T.K16[:], T.PF[:, 1:2], -2 * BIG, A.is_equal, A.mult, ["K16", "PF"], ["XB"])
-    ts("v", T.RO[:], T.QP[:, 0:K], 0.0, T.PF[:, 0:1], A.mult, A.add, ["QP", "PF"], ["RO"])
+    ts(T.UO[:, 16:24], T.K16[:, 0:8], 16.0, T.PF[:, 4:5], A.mult, A.add, ["K16", "PF"], ["UO1"])
+    ts(T.XA[:], T.K16[:], T.PF[:, 0:1], BIG, A.is_equal, A.mult, ["K16", "PF"], ["XA"])
+    ts(T.XB[:], T.K16[:], T.PF[:, 1:2], -2 * BIG, A.is_equal, A.mult, ["K16", "PF"], ["XB"])
+    ts(T.RO[:], T.QP[:, 0:K], 0.0, T.PF[:, 0:1], A.mult, A.add, ["QP", "PF"], ["RO"])
     tt(T.XC[:], T.XA[:], T.XB[:], A.add, ["XA", "XB"], ["XC"])
     cp("s", T.XP[:], T.XC[:].indirect(T.RO[:]), ["XC", "RO"], ["XP"])
     quant("UQ", "US", 0, 128, T.UB[:], ["UB"], ["UQ"])
     cp("s", T.UPS[:], T.US[:].indirect(T.UO[:]), ["UQ", "UO0", "UO1"], ["UPS"])
-    ts("v", T.TR[:], T.I3[:], T.PF[:, 2:3], -0.5, A.is_gt, A.mult, ["I3", "PF"], ["TR"])
+    ts(T.TR[:], T.I3[:], T.PF[:, 2:3], -0.5, A.is_gt, A.mult, ["I3", "PF"], ["TR"])
     cp("v", T.UP[:].bitcast(dt.uint32), T.UQ[:].bitcast(dt.uint32).indirect(T.UO[:]), ["UQ", "UO0", "UO1"], ["UP"])
     act(T.XO[:, 6:7], T.XA[:, 0:1], AF.Identity, ["XA"], ["XO6"], bias=-BIG - 1.0, scale=2.0)
     act(T.XO[:, 0:5], T.K16[:, 0:5], AF.Identity, ["K16", "XO6"], ["XO"], bias=T.XO[:, 6:7], scale=0.5)
     act(T.XO[:, 5:6], T.XC[:, 15:16], AF.Identity, ["XC", "XO"], ["XO5"], bias=T.XO[:, 4:5])
-    for j in range(NG):
+    for j in range(NB // 2):
         for side in "lrd":
             for k in slots("G%d" % j, side):
                 writer[k] = []
-
-    def state(t, k):
-        a, b = runs(TC[t])[k]
-        quant("TQ%d" % t, "TS%d" % t, a, b, T["X%d" % t][:, 4 * a:4 * b], slots("X%d" % t, k), ["TQ%d_%d" % (t, a)])
-
-    def signs(t, b, side="ab"):
-        sg, buys, cut = "SG%d" % (b % NSG), rank < rank ^ STEP[t], TC[t][1]
-        a0, a1 = cut if side == "b" else 0, cut if side == "a" else DIRECT.get(b, C)
-        for h in range(2):
-            c, bank = 2 * b + h, ps((P if side == "a" else Q)[h])
-            p, pn = (T.ST[:, 16 * c:16 * c + 1], "ST") if buys else (T.PN[:, c:c + 1], "PN")
-            act(T[sg][:, 2 * a0 + h:2 * a1:2], T[bank][:, a0:a1], AF.Sign, [bank, pn + str(int(32 * b >= cut))],
-                [sg + "_%d%s" % (h, s) for s in side] + [sg + "d"] * ((1 - h) * ("a" in side)),
-                bias=p, scale=-1.0 if buys else 1.0)
-
     state(0, 0)
-    scores(0, 0)
+    for name in ("s0", "e0", "e1"):
+        product(0, name)
     state(0, 1)
-    turn(0, 0, rank > rank ^ STEP[0])
-    for b in range(EARLY[0]):
-        signs(0, b, "a")
-    ts("v", T.CB[:], T.I2[:], T.PF[:, 3:4], None, A.is_equal, None, ["I2", "PF"], ["CB"])
-    ts("v", T.XD[:], T.K16[:], T.PF[:, 5:6], 8.0, A.add, A.is_equal, ["K16", "PF"], ["XD"])
+    turn(0, 0)
+    early(0)
+    ts(T.CB[:], T.I2[:], T.PF[:, 3:4], None, A.is_equal, None, ["I2", "PF"], ["CB"])
+    ts(T.XD[:], T.K16[:], T.PF[:, 5:6], 8.0, A.add, A.is_equal, ["K16", "PF"], ["XD"])
     quant("CQ", "CS", 0, 128, T.CB[:], ["CB"], ["CQ"])
+    for b in range(AHEAD[0]):
+        ahead(0, b)
 
     for t in range(2):
-        mate = rank ^ STEP[t]
-        dst = T.cores[mate]
-        buys = rank < mate
+        dst = T.cores[rank ^ STEP[t]]
         n = str(t)
         XN, NQ, NS = "X" + str(t + 1), "TQ" + str(t + 1), "TS" + str(t + 1)
         TQ, TS, LQ, LS = "TQ" + n, "TS" + n, "LQ" + n, "LS" + n
         SO, SP, LO, LP, MK, AO = "SO" + n, "SP" + n, "LO" + n, "LP" + n, "MK" + n, "AO" + n
         whole = parts(TQ, TC[t])
-        scores(t, 1)
+        mine, theirs = P[2:] + Q[:2], Q[2:] + P[:2]
+        for name in SECOND:
+            product(t, name)
         send(dst, "rT" + n, [(T[LQ][:].bitcast(dt.uint8), T[TQ][:].bitcast(dt.uint8), whole, [LQ]),
                              (T[LS][:], T[TS][:], whole, [LS])])
         iota(MK, T[MK][:], [[0, UN]], 0, 0)
@@ -302,103 +357,71 @@ def rank_program(g, core, T, topo):
                 iota("HPz%d" % b, T.HP[:, HW * b + C:HW * b + HW], [[0, HW - C]], 0, 0)
             iota("IOz", T.IO[:, C:HW], [[0, HW - C]], -1, 0)
 
-        def pack(i):
-            j, last = str(i % NG), i == NB // 2 - 1
-            gq, gs, rd = "GQ" + j, "GS" + j, [k for side in "lrd" for k in slots("G" + j, side)]
-            if not last:
-                quant(gq, gs, 0, C, T["G" + j][:], rd, parts(gq, UC))
-            for k, (a, b) in enumerate(runs(UC)):
-                if last:
-                    quant(gq, gs, a, b, T["G" + j][:, 4 * a:4 * b], rd, [gq + "_%d" % a])
-                mm(P[k], "CQ", "CS", 0, gq, gs, i == 0, last, ["CQ", gq + "_%d" % a], a, b)
+        def signs(b):
+            if b not in DIRECT[t]:
+                for h in range(2):
+                    sign(t, b, h, "b" if b < EARLY[t] else "ab")
 
-        def ties(b):
-            sg, s = "SG%d" % (b % NSG), "ab"[32 * b >= TC[t][1]]
-            d = T[sg][:, 64 * b:64 * b + 64]
-            tt(d, d, T.TR[:], A.is_gt, [sg + "_0" + s, sg + "_1" + s, "TR"], [sg + "d"])
-
-        def weigh(b, side):
-            sg, gn, e, cut = "SG%d" % (b % NSG), "G%d" % (b // 2 % NG), 32 * b + 32, TC[t][1]
-            reach = "ab" if (side == "r") == (e <= cut) else "b" if side == "r" else "a"
-            for h in range(2):
-                k, c = 2 * (b % 2) + h, 4 * (2 * b + h) + 3
-                w = T.Q4[:, c:c + 1]
-                names = ([sg + "_%d%s" % (h, s) for s in reach] + ["Q4%d" % (e > cut)], [gn + "_%d%s" % (k, side)])
-                end = DIRECT.get(b, C)
-                if side == "d":
-                    bank = ps((P, Q)[h][3])
-                    ts("v", T[gn][:, 4 * end + k:4 * C:4], T[bank][:, end:C], T.ST[:, 4 * c - 12:4 * c - 11], w,
-                       A.is_le if buys else A.is_ge, A.mult, [bank, "ST%d" % (e > cut), names[0][-1]], names[1])
-                    continue
-                if side == "r":
-                    if e < end:
-                        ts("v", T[gn][:, 4 * e + k:4 * end:4], T[sg][:, 2 * e + h:2 * end:2], 0.0, w, A.is_ge, A.mult, *names)
-                    continue
-                names[0].append(sg + "d")
-                if b in SCALAR_LEFT:
-                    part = int(e > cut)
-                    if part not in widened:
-                        a0, a1 = runs(TC[t])[part]
-                        cp("s", T.QS[:, a0 // 16:a1 // 16], T.Q4[:, a0 // 4 + 3:a1 // 4:4], ["Q4%d" % part], ["QS%d" % part])
-                        widened.append(part)
-                    act(T[gn][:, k:4 * e:4], T[sg][:, h:2 * e:2], AF.Relu, names[0] + ["QS%d" % part], names[1],
-                        scale=T.QS[:, c // 4:c // 4 + 1])
-                else:
-                    ts("v", T[gn][:, k:4 * e:4], T[sg][:, h:2 * e:2], 0.0, w, A.is_gt, A.mult, *names)
-
-        last = NB - 1
-        ready = [0] * (NB // 2)
+        packed, left = 0, list(range(AHEAD[t]))
+        signs(0)
+        if AHEAD[t] == 0:
+            ties(t, 0)
         for b in range(NB):
-            ready[b // 2] = max(ready[b // 2], b + 1 + (DELAY if b in SCALAR_LEFT else 0))
-        packed, widened = 0, []
-        signs(t, 0, "b" if EARLY[t] else "ab")
-        for b in range(NB):
-            if b in DIRECT:
-                weigh(b, "d")
+            if b in DIRECT[t]:
+                weigh(t, b, "d")
             if b + 1 < NB:
-                signs(t, b + 1, "b" if b + 1 < EARLY[t] else "ab")
-            if b - DELAY in SCALAR_LEFT:
-                weigh(b - DELAY, "l")
-            if not (b == last and last in SCALAR_LEFT):
-                ties(b)
-            if b == last - 1 and last in SCALAR_LEFT:
-                ties(last)
-                weigh(last, "l")
-            while packed < NB // 2 - 1 and ready[packed] <= b:
+                signs(b + 1)
+            for c in SCALAR_LEFT:
+                if c not in left and c + DELAY <= b:
+                    weigh(t, c, "l")
+                    left.append(c)
+            if AHEAD[t] <= b + 1 < NB:
+                ties(t, b + 1)
+            if b + 2 == NB:
+                for c in SCALAR_LEFT:
+                    if c not in left:
+                        weigh(t, c, "l")
+                        left.append(c)
+            if b >= AHEAD[t]:
+                weigh(t, b, "r")
+            elif b not in DIRECT[t]:
+                weigh(t, b, "e")
+            if b % 2 == 0 and AHEAD[t] <= b + 1:
+                need("v", writer["SG%dd" % (b + 1)][0])
+            while packed < b // 2 and 2 * packed in left and 2 * packed + 1 in left:
                 pack(packed)
                 packed += 1
-            weigh(b, "r")
-            if b not in SCALAR_LEFT:
-                weigh(b, "l")
-            if b == 0:
-                turn(t, 1, not buys)
-            if t > 0 and b == max([0] + list(DIRECT)):
-                unpack(P[2:] + Q[2:], TQ, TS, whole, True, True)
+            if b not in SCALAR_LEFT and b not in left:
+                weigh(t, b, "l")
+                left.append(b)
+            if b == TURN:
+                turn(t, 1)
+            if t > 0 and b == EARLY[t]:
+                unpack(mine, TQ, TS, whole, True, True)
         pack(NB // 2 - 1)
         for k, (a, b) in enumerate(runs(UC)):
             c, d = a // 16, b // 16
             wrap("EX", T[ps(P[k])][:, 0:b - a], [ps(P[k])], ["EX_%d" % a], a, b, "XP")
-            ts("v", T[SO][:, c:d], T.EX[:, a + 15:b:16], T.XO[:, 2:3], None, A.add, None, ["EX_%d" % a, "XO"], [SO + "_%d" % a])
+            ts(T[SO][:, c:d], T.EX[:, a + 15:b:16], T.XO[:, 2:3], None, A.add, None, ["EX_%d" % a, "XO"], [SO + "_%d" % a])
             send(dst, "rS%d%d" % (t, k), [(T[SP][:, c:d], T[SO][:, c:d], [SO + "_%d" % a], [SP + "_%d" % a])])
 
         def mark(name, a, b):
-            cp("v", T[MK][:].indirect(T[name][:, a // 16:b // 16]), T.ONE[:, a:b],
-               [name + "_%d" % c for c in UC[:-1] if a <= c < b] + ["ONE"], [MK])
+            cp("v", T[MK][:].indirect(T[name][:, a // 16:b // 16]), T.ONE[:, a:b], parts(name, UC, a, b) + ["ONE"], [MK])
 
-        ts("v", T.GO[:], T.EX[:, 15:C:16], T.XO[:, 3:4], 0.5, A.add, A.mult, parts("EX", UC) + ["XO"], ["GO"])
+        ts(T.GO[:], T.EX[:, 15:C:16], T.XO[:, 3:4], 0.5, A.add, A.mult, parts("EX", UC) + ["XO"], ["GO"])
         mark(SO, 0, C)
         if t == 0:
-            ts("v", T.XF[:], T.XD[:], -2 * BIG, -AGE, A.mult, A.add, ["XD"], ["XF"])
+            ts(T.XF[:], T.XD[:], -2 * BIG, -AGE, A.mult, A.add, ["XD"], ["XF"])
             for b in range(4):
                 quant("EQ", "ES", 128 * b, 128 * b + 128, T.EB[:, 3 - b:515 - b], ["EB"], ["EQ_%d" % b])
             tt(T.XG[:], T.XF[:], T.XA[:], A.add, ["XA", "XF"], ["XG"])
-            unpack(P[2:] + Q[2:], TQ, TS, whole, True, True)
-        ts("v", T.EO[:], T.GO[:], -2.0, T.XO[:, 5:6], A.mult, A.add, ["GO", "XO5"], ["EO"])
+            unpack(mine, TQ, TS, whole, True, True)
+        ts(T.EO[:], T.GO[:], -2.0, T.XO[:, 5:6], A.mult, A.add, ["GO", "XO5"], ["EO"])
         tt(T.XE[:, 15:C:16], T.EX[:, 15:C:16], T.EO[:], A.add, parts("EX", UC) + ["EO"], ["XE"])
         mark(SP, *runs(UC)[0])
-        unpack(Q[:2] + P[:2], LQ, LS, [LQ, LS], True, True)
-        halves = [("DO", b, bank) for b, bank in enumerate(P[2:] + Q[2:])] + [("DP", b, bank) for b, bank in enumerate(Q[:2] + P[:2])]
-        for i, (name, b, bank) in enumerate(halves):
+        unpack(theirs, LQ, LS, [LQ, LS], True, True)
+        (a0, cut), (cut, a1) = runs(TC[t + 1])
+        for i, bank in enumerate(mine + theirs):
             if i == BEFORE[t]:
                 for a, c in runs(UC)[1:]:
                     mark(SP, a, c)
@@ -408,70 +431,81 @@ def rank_program(g, core, T, topo):
                        T.SEG[:, 0:UN // 2 + 1].indirect(T.GO[:, K // 2 * k:K // 2 * (k + 1)]), ["SEG", "GO"], ["FR%d" % k])
                 if t == 0:
                     cp("s", T.XH[:], T.XG[:].indirect(T.RO[:]), ["XG", "RO"], ["XH"])
+            name, b = ("DO", "DP")[i // 4], i % 4
             act(T[name][:, C * b:C * b + C], T[ps(bank)][:, 0:C], AF.Copy, [ps(bank)], [name + "_%d" % b], scale=0.5)
-        unpack(P, TQ, TS, whole, True, False, *runs(TC[t + 1])[0])
+            if i < 4:
+                cp("s", T.DT[:, C * b + cut:C * b + C], T[ps(bank)][:, cut:C], [ps(bank)], ["DT_%d" % b])
+        unpack(P, TQ, TS, whole, True, False, 0, cut)
         wrap("EY", T.FR[:], ["FR0", "FR1"], ["EY"], 0, C, "XE")
-        ts("v", T.FS[:], T.EY[:, 15:C:16], T.XO[:, 0:1], None, A.add, None, ["EY", "XO"], ["FS"])
+        ts(T.FS[:], T.EY[:, 15:C:16], T.XO[:, 0:1], None, A.add, None, ["EY", "XO"], ["FS"])
         cp("v", T[AO][:].indirect(T.FS[:]), T.IO[:, 0:C], ["FS", "IO"], [AO])
-        for k, (a, b) in enumerate(runs(ZC)):
+        for k, (a, b) in enumerate(runs(LC)):
             c, d, e = a // 16, b // 16, "_%d" % a
-            wrap("EZ", T[AO][:, a:b], [AO] + ["EZ_%d" % ZC[k - 1]] * (k > 0), ["EZ" + e], a, b, "XH",
+            wrap("EZ", T[AO][:, a:b], [AO] + ["EZ_%d" % LC[k - 1]] * (k > 0), ["EZ" + e], a, b, "XH",
                  T.EZ[:, a - 1:a] if k else float(LOW))
             tt(T.LI[:, c:d], T.EZ[:, a + 7:b:16], T.EZ[:, a + 15:b:16], A.max, ["EZ" + e], ["LI" + e])
-            ts("v", T.LJ[:, c:d], T.LI[:, c:d], int(AGE) - 1, None, A.bitwise_and, None, ["LI" + e], ["LJ" + e])
+            ts(T.LJ[:, c:d], T.LI[:, c:d], int(AGE) - 1, None, A.bitwise_and, None, ["LI" + e], ["LJ" + e])
             cp("v", T[LO][:, c:d], T.LJ[:, c:d], ["LJ" + e], [LO + e])
             send(dst, "rL%d%d" % (t, k), [(T[LP][:, c:d], T[LO][:, c:d], [LO + e], [LP + e])])
-        ts("v", T.FO[:], T.EY[:, 15:C:16], T.XO[:, 0:1], float(C), A.add, A.min, ["EY", "XO"], ["FO"])
-        if t == 1:
-            quant("VQ", "VS", 0, 128, T.VB[:], ["VB"], ["VQ"])
-
-        def own_parts(k):
-            a, b = runs(ZC)[k]
+        ts(T.FO[:], T.EY[:, 15:C:16], T.XO[:, 0:1], float(C), A.add, A.min, ["EY", "XO"], ["FO"])
+        for k, (a, b) in enumerate(runs(LC)):
             for i in range(4):
                 cp(OWN_ON[k][i], T.ZT[:, C * i + a:C * i + b], T.DO[:, C * i:C * i + C].indirect(T[LO][:, a // 16:b // 16]),
-                   ["DO_%d" % i, LO + "_%d" % a], ["ZT_%d%d" % (i, k)])
+                   ["DO_%d" % i, LO + "_%d" % a], ["ZT%d_%d" % (i, a)])
+        if t == 1:
+            quant("VQ", "VS", 0, 128, T.VB[:], ["VB"], ["VQ"])
+            cp("s", T.OL[:], T.IO[:].indirect(T.FO[:]), ["IO", "IOz", "FO"], ["OL"])
+            dma("y", "dol", [(T.ol[:], T.OL[0:128:16, :], ["OL"], [])])
 
-        def relu(k):
-            a, b = runs(ZC)[k]
-            for i, bank in enumerate(Q):
-                out, src, names = T.HP[:, HW * i + a:HW * i + b], T[ps(bank)][:, 0:b - a], ([ps(bank)], ["HP_%d%d" % (i, k)])
-                if RELU_ON[k][i] == "v":
-                    ts("v", out, src, 0.0, 0.03125, A.max, A.mult, *names)
-                else:
-                    act(out, src, AF.Relu, *names, scale=0.03125)
+        def pick(k, i):
+            a, b = runs(TC[t + 1])[k]
+            cp(PICK_ON[k][i], T.HT[:, 4 * a + i:4 * b:4], T.HP[:, HW * i:HW * i + HW].indirect(T.FO[:, a // 16:b // 16]),
+               parts("HP%d" % i, ZC) + ["HPz%d" % i, "FO"], ["HT_%d%d" % (i, k)])
 
-        for k in range(len(ZC) - 1):
-            own_parts(k)
-        for k, (a, b) in enumerate(runs(ZC)):
+        for a, b in runs(ZC):
             for i in range(4):
                 tt(T.Z[:, 4 * a + i:4 * b:4], T.DP[:, C * i:C * i + C].indirect(T[LP][:, a // 16:b // 16]),
-                   T.ZT[:, C * i + a:C * i + b], A.add, ["DP_%d" % i, LP + "_%d" % a, "ZT_%d%d" % (i, k)], ["Z_%d%d" % (i, k)])
-            quant("ZQ", "ZS", a, b, T.Z[:, 4 * a:4 * b], slots("Z", k), ["ZQ_%d" % a])
-            for i, bank in enumerate(Q):
-                mm(bank, "WQ", "WS", 128 * i, "ZQ", "ZS", True, True, ["WQ", "WS", "ZQ_%d" % a], a, b)
-            relu(k)
-            if t == 1 and k == 0:
-                cp("s", T.OL[:], T.IO[:].indirect(T.FO[:]), ["IO", "IOz", "FO"], ["OL"])
-                dma("y", "dol", [(T.ol[:], T.OL[0:128:16, :], ["OL"], [])])
-        unpack(Q, TQ, TS, whole, True, False, *runs(TC[t + 1])[1])
-        for k, (a, b) in enumerate(runs(TC[t + 1])):
+                   T.ZT[:, C * i + a:C * i + b], A.add, ["DP_%d" % i] + parts(LP, LC, a, b) + parts("ZT%d" % i, LC, a, b),
+                   ["Z_%d_%d" % (i, a)])
+            quant("ZQ", "ZS", a, b, T.Z[:, 4 * a:4 * b], slots("Z", "_%d" % a), ["ZQ_%d" % a])
             for i in range(4):
-                cp(PICK_ON[k][i], T.HT[:, 4 * a + i:4 * b:4], T.HP[:, HW * i:HW * i + HW].indirect(T.FO[:, a // 16:b // 16]),
-                   ["HP_%d%d" % (i, j) for j in range(len(ZC) - 1)] + ["HPz%d" % i, "FO"], ["HT_%d%d" % (i, k)])
-            quant("HQ", "HS", a, b, T.HT[:, 4 * a:4 * b], slots("HT", k), ["HQ_%d" % a])
-            unpack((P, Q)[k], "HQ", "HS", ["HQ_%d" % a], False, True, a, b)
-        for k, (a, b) in enumerate(runs(TC[t + 1])):
-            for i, bank in enumerate((P, Q)[k]):
-                cp(STATE_ON[k][i], T[XN][:, 4 * a + i:4 * b:4], T[ps(bank)][:, 0:b - a], [ps(bank)], [XN + "_%d%d" % (i, k)])
-            state(t + 1, k)
-            if t == 1:
-                mm((P, Q)[k][0], "VQ", "VS", 0, NQ, NS, True, True, ["VQ", NQ + "_%d" % a], a, b)
-            elif k == 0:
-                scores(1, 0)
-            else:
-                turn(1, 0, rank > rank ^ STEP[1])
-                for b in range(EARLY[1]):
-                    signs(1, b, "a")
+                mm(Q[i], "WQ", "WS", 128 * i, "ZQ", "ZS", True, True, ["WQ", "WS", "ZQ_%d" % a], a, b)
+            for i in range(4):
+                out, src, names = T.HP[:, HW * i + a:HW * i + b], T[ps(Q[i])][:, 0:b - a], ([ps(Q[i])], ["HP%d_%d" % (i, a)])
+                if b == C and PICK_ON[0][i] == "v":
+                    ts(out, src, 0.0, 0.03125, A.max, A.mult, *names)
+                else:
+                    act(out, src, AF.Relu, *names, scale=0.03125)
+                if b == C:
+                    pick(0, i)
+        quant("HQ", "HS", 0, cut, T.HT[:, 0:4 * cut], slots("HT", 0), ["HQ_0"])
+        unpack(P, "HQ", "HS", ["HQ_0"], False, True, 0, cut)
+        for i in range(4):
+            pick(1, i)
+        quant("HQ", "HS", cut, C, T.HT[:, 4 * cut:4 * C], slots("HT", 1), ["HQ_1"])
+        for i in range(4):
+            cp("s", T[XN][:, i:4 * cut:4], T[ps(P[i])][:, 0:cut], [ps(P[i])], [XN + "_%d0" % i])
+        state(t + 1, 0)
+        for name in OPENING:
+            i = int(name[1])
+            if name[0] == "x":
+                unpack(Q, "HQ", "HS", ["HQ_1"], True, True, cut, C, [i])
+                tt(T[XN][:, 4 * cut + i:4 * C:4], T[ps(Q[i])][:, 0:C - cut], T.DT[:, C * i + cut:C * i + C], A.add,
+                   [ps(Q[i]), "DT_%d" % i], [XN + "_%d1" % i])
+            elif t == 0:
+                product(1, name)
+                if name == "s0":
+                    turn(1, 0)
+                if name == "e1":
+                    early(1)
+                    for b in range(FIRST):
+                        ahead(1, b)
+        state(t + 1, 1)
+        if t == 0:
+            for b in range(FIRST, AHEAD[1]):
+                ahead(1, b)
+    for k, (a, b) in enumerate(runs(TC[2])):
+        mm((P, Q)[k][0], "VQ", "VS", 0, NQ, NS, True, True, ["VQ", NQ + "_%d" % a], a, b)
 
     def store(e, out, in_, rd):
         order(e, rd, [], False)

from concourse.mybir import dt, AluOpType, ActivationFunctionType

C = 448
K = C // 16
NB = C // 32
UN = 4 * C
HW = C + 16
BIG = float(2 ** 19)
LOW = -(2 ** 20)
AGE = 512.0
STEP = [1, 2]
TC = [[0, 224, C], [0, 224, C], [0, 224, C]]
UC = [0, 160, C]
LC = [0, 160, C]
ZC = [0, 160, 320, C]
EARLY = [3, 4]
AHEAD = [2, 3]
FIRST = 0
DIRECT = [[0, 1], [0, 1]]
SCALAR_LEFT = [13]
DELAY = 2
OPENING = ["x0", "x1", "s0", "e0", "e1", "x2", "x3"]
SECOND = ["f0", "g0", "f1", "g1", "s1"]
BEFORE = [2, 5]
OWN_ON = ["ssss", "ssss"]
PICK_ON = ["svsv", "svsv"]
SHARE = False
TURN = 1
P, Q = [0, 1, 2, 3], [4, 5, 6, 7]

F32, BF, I32, U16, CODE, U8 = "float32", "bfloat16", "int32", "uint16", "float8_e4m3fn_x4", "uint8"
SCRATCH = {}
for _n, _w, _d in [
        ("X0", 4 * C, BF), ("X1", 4 * C, BF), ("X2", 4 * C, BF), ("UB", 512, BF), ("VB", 512, BF),
        ("UQ", 128, CODE), ("US", 128, U8), ("UP", 384, CODE), ("UPS", 384, U8), ("VQ", 128, CODE), ("VS", 128, U8),
        ("WQ", 512, CODE), ("WS", 512, U8), ("EB", 516, BF), ("EQ", 512, CODE), ("ES", 512, U8),
        ("CB", 512, BF), ("CQ", 128, CODE), ("CS", 128, U8),
        ("I2", 512, BF), ("I3", 64, F32), ("PI", 2, I32), ("PJ", 6, I32), ("PF", 6, F32),
        ("UI", 24, F32), ("UO", 24, U16), ("K16", 16, F32), ("XA", 16, F32), ("XB", 16, F32), ("XC", 16, F32),
        ("XD", 16, F32), ("XF", 16, F32), ("XG", 16, F32),
        ("RO", K, U16), ("XP", C, F32), ("XE", C, F32), ("XH", C, F32), ("XO", 8, F32), ("TR", 64, BF),
        ("QP", C // 4, F32), ("IO", HW, F32), ("ONE", 516, BF),
        ("TQ0", C, CODE), ("TS0", C, U8), ("TQ1", C, CODE), ("TS1", C, U8), ("TQ2", C, CODE), ("TS2", C, U8),
        ("LQ0", C, CODE), ("LS0", C, U8), ("LQ1", C, CODE), ("LS1", C, U8),
        ("ST", C, F32), ("QF", C // 4, F32), ("Q4", C // 4, BF), ("QS", K, F32), ("PN", K, F32),
        ("EX", C, F32), ("EY", C, F32), ("EZ", C, F32), ("FR", C, F32),
        ("SO0", 32, U16), ("SO1", 32, U16), ("SP0", 32, U16), ("SP1", 32, U16),
        ("LO0", 32, U16), ("LO1", 32, U16), ("LP0", 32, U16), ("LP1", 32, U16),
        ("FO", K, U16), ("FS", K, U16), ("LI", K, I32), ("LJ", K, I32), ("EO", K, F32), ("GO", K, U16),
        ("MK0", UN, BF), ("MK1", UN, BF), ("SEG", UN // 2 + 16, F32), ("AO0", 2 * C, F32), ("AO1", 2 * C, F32),
        ("DO", 4 * C, BF), ("DP", 4 * C, BF), ("DT", 4 * C, BF), ("ZT", 4 * C, BF), ("Z", 4 * C, BF),
        ("ZQ", C, CODE), ("ZS", C, U8),
        ("HP", 4 * HW, BF), ("HT", 4 * C, BF), ("HQ", C, CODE), ("HS", C, U8), ("YS", C, F32), ("OL", C, F32)]:
    SCRATCH[_n] = ("sbuf", [128, _w], _d)
for _n, _w, _d in [("SG", 2 * C * NB, BF), ("G", 2 * C * NB, BF), ("GQ", C * NB // 2, CODE), ("GS", C * NB // 2, U8)]:
    SCRATCH[_n] = ("sbuf", [128, _w], _d)
for _i in range(8):
    SCRATCH["ps%d" % _i] = ("psum", [128, 512], F32)
SEMAPHORES = (["cv", "cs", "ct", "cg", "dx0", "dx1", "du", "dv", "dw", "dol", "sent", "rT0", "rT1", "dst"]
              + ["rS%d%d" % (_t, _k) for _t in range(2) for _k in range(len(UC) - 1)]
              + ["rL%d%d" % (_t, _k) for _t in range(2) for _k in range(len(LC) - 1)])

A = AluOpType
AF = ActivationFunctionType


def runs(edges):
    return list(zip(edges[:-1], edges[1:]))


def rank_program(g, core, T, topo):
    rank = T.rank_of(core)
    if rank is None:
        return
    q = {"v": g.vector, "s": g.scalar, "t": g.tensor, "g": g, "y": g.sync}
    own = {"v": "cv", "s": "cs", "t": "ct", "g": "cg"}
    total = {n: 0 for n in SEMAPHORES}
    waited = {n: 0 for n in SEMAPHORES}
    clock = {e: {} for e in q}
    snap, writer, readers = {}, {}, {}

    def need(e, tok):
        s, n = tok
        if clock[e].get(s, 0) >= n:
            return
        q[e].wait_ge(T.sem[s], n)
        waited[s] = max(waited[s], n)
        for k, m in list(snap.get(tok, {}).items()) + [(s, n)]:
            clock[e][k] = max(clock[e].get(k, 0), m)

    def order(e, rd, wr, acc):
        toks = []
        for k in rd:
            toks += writer[k]
            if k.startswith("ps"):
                toks += [t for f, t in readers.get(k, []) if f != e]
        for k in wr:
            if not acc:
                toks += writer.get(k, [])
            toks += [t for f, t in readers.get(k, [])]
        best = {}
        for s, n in toks:
            best[s] = max(best.get(s, 0), n)
        for s in sorted(best, key=lambda s: -len(snap.get((s, best[s]), {}))):
            need(e, (s, best[s]))

    def done(e, tok, rd, wr):
        snap[tok] = dict(clock[e])
        for k in rd:
            readers.setdefault(k, []).append((e, tok))
        for k in wr:
            writer[k] = [tok]
            readers[k] = []

    def op(e, call, rd, wr, acc=False):
        order(e, rd, wr, acc)
        s = own[e]
        call(q[e]).then_inc(T.sem[s], 1)
        total[s] += 1
        done(e, (s, total[s]), rd, wr)

    def dma(e, sem, items):
        tok = (sem, total[sem] + 16 * len(items))
        for out, in_, rd, wr in items:
            order(e, rd, wr, False)
            q[e].dma_start(out, in_).then_inc(T.sem[sem], 16)
        total[sem] = tok[1]
        for out, in_, rd, wr in items:
            done(e, tok, rd, wr)

    def send(dst, sem, items):
        rid, pid, se = topo.addr(dst)
        m = topo.mask(core, dst)
        n = len(topo.engines(core, dst))
        for out, in_, rd, land in items:
            order("g", rd, [], False)
            g.remote_dma(out, in_, T.sem[sem], T.sem["sent"], pid, rid, m)
            total["sent"] += n
            total[sem] += len(topo.engines(dst, core))
        for out, in_, rd, land in items:
            for k in land:
                writer[k] = [(sem, total[sem])]

    def ts(out, in0, s1, s2, o0, o1, rd, wr):
        if s2 is None:
            op("v", lambda E: E.tensor_scalar(out, in0, s1, None, o0), rd, wr)
        else:
            op("v", lambda E: E.tensor_scalar(out, in0, s1, s2, o0, o1), rd, wr)

    def tt(out, a, b, o, rd, wr):
        op("v", lambda E: E.tensor_tensor(out, a, b, o), rd, wr)

    def act(out, in_, f, rd, wr, **kw):
        op("s", lambda E: E.activation(out, in_, f, **kw), rd, wr)

    def cp(e, out, in_, rd, wr):
        if e == "v":
            op(e, lambda E: E.tensor_copy(out, in_), rd, wr)
        else:
            act(out, in_, AF.Copy, rd, wr)

    def fill(out, val, wr):
        op("v", lambda E: E.memset(out, val), [], wr)

    def iota(name, out, pat, base, cm, ints=False):
        if ints:
            op("g", lambda E: E.iota(out, pat, base, cm), [], [name])
        else:
            op("g", lambda E: E.iota(out, pat, base, cm, allow_small_or_imprecise_dtypes=True), [], [name])

    def quant(qn, sn, a, b, src, rd, wr):
        op("v", lambda E: E.quantize_mx(T[qn][:, a:b], T[sn][:, a:b], src), rd, wr)

    def ps(bank):
        return "ps%d" % bank

    def mm(bank, wq, ws, wa, xq, xs, start, stop, rd, a=0, b=C):
        op("t", lambda E: E.matmul_mx(T[ps(bank)][:, 0:b - a], T[wq][:, wa:wa + 128], T[ws][:, wa:wa + 128],
                                      T[xq][:, a:b], T[xs][:, a:b], start, stop), rd, [ps(bank)], acc=not start)

    def scan(out, d0, d1, init, o0, o1, rd, wr):
        op("v", lambda E: E.tensor_tensor_scan(out, d0, d1, init, o0, o1), rd, wr)

    def wrap(dst, src, rd, wr, a, b, pattern, init=float(LOW)):
        scan(T[dst][:, a:b], src, T[pattern][:, a:b], init, A.max, A.add, rd + [pattern], wr)

    def slots(n, k=""):
        return [n + "_%d%s" % (b, k) for b in range(4)]

    def parts(n, edges, a=0, b=C):
        return [n + "_%d" % c for c, d in runs(edges) if c < b and d > a]

    def unpack(banks, qn, sn, rd, start, stop, a=0, b=C, planes=range(4)):
        for i in planes:
            mm(banks[i], "EQ", "ES", 128 * i, qn, sn, start, stop, ["EQ_%d" % i] + rd, a, b)

    def buyer(t):
        return rank < rank ^ STEP[t]

    def state(t, k):
        a, b = runs(TC[t])[k]
        quant("TQ%d" % t, "TS%d" % t, a, b, T["X%d" % t][:, 4 * a:4 * b], slots("X%d" % t, k), ["TQ%d_%d" % (t, a)])

    def product(t, name):
        kind, i, cut = name[0], int(name[1]), TC[t][1]
        bank, wa = (P[2 + i], 256) if kind == "s" else ({"e": P, "g": Q, "f": Q[2:]}[kind][i], 128 * i)
        a, b = (0, C) if kind == "f" else (cut, C) if name in ("s1", "g0", "g1") else (0, cut)
        if kind in "sf" or EARLY[t]:
            mm(bank, "UP", "UPS", wa, "TQ%d" % t, "TS%d" % t, True, True, ["UP", "UPS"] + parts("TQ%d" % t, TC[t], a, b), a, b)

    def turn(t, k):
        a, b = runs(TC[t])[k]
        bank = ps(P[2 + k])
        op("v", lambda E: E.transpose(T.ST[:, a:b], T[bank][:, 0:b - a]), [bank], ["ST%d" % k])
        if not buyer(t):
            ts(T.PN[:, a // 16:b // 16], T.ST[:, a:b:16], -1.0, None, A.mult, None, ["ST%d" % k], ["PN%d" % k])
        ts(T.QF[:, a // 4:b // 4], T.ST[:, a:b:4], 0.0, None, A.is_gt, None, ["ST%d" % k], ["QF%d" % k])
        scan(T.Q4[:, a // 4:b // 4], T.QP[:, a // 4:b // 4], T.QF[:, a // 4:b // 4], 1.0, A.min, A.add,
             ["QP", "QF%d" % k], ["Q4%d" % k])

    def sign(t, b, h, side):
        sg, cut, c, s0 = "SG%d" % b, TC[t][1], 2 * b + h, 2 * C * b
        a0, a1 = cut if side == "b" else 0, cut if side == "a" else C
        bank = ps({"a": P, "b": Q if SHARE else Q[2:], "ab": Q[2:]}[side][h])
        o = cut if side == "b" and SHARE else 0
        p, pn = (T.ST[:, 16 * c:16 * c + 1], "ST") if buyer(t) else (T.PN[:, c:c + 1], "PN")
        act(T.SG[:, s0 + 2 * a0 + h:s0 + 2 * a1:2], T[bank][:, a0 - o:a1 - o], AF.Sign, [bank, pn + str(int(32 * b >= cut))],
            [sg + "_%d%s" % (h, s) for s in side] + [sg + "d"] * ((1 - h) * ("a" in side)),
            bias=p, scale=-1.0 if buyer(t) else 1.0)

    def ties(t, b):
        sg, s = "SG%d" % b, "ab"[32 * b >= TC[t][1]]
        d = T.SG[:, (2 * C + 64) * b:(2 * C + 64) * b + 64]
        tt(d, d, T.TR[:], A.is_gt, [sg + "_0" + s, sg + "_1" + s, "TR"], [sg + "d"])

    def weigh(t, b, side):
        sg, gn, e, cut = "SG%d" % b, "G%d" % (b // 2), 32 * b + 32, TC[t][1]
        s0, g0 = 2 * C * b, 4 * C * (b // 2)
        part, end = int(e > cut), cut if b in DIRECT[t] or b < AHEAD[t] else C
        if side == "e":
            side, e, end = "r", cut, C
        reach = "ab" if (side == "l" and part) or (side == "r" and e < cut < end) else "b" if e >= cut and side == "r" else "a"
        for h in range(2):
            k, c = 2 * (b % 2) + h, 2 * b + h
            w, wr = T.Q4[:, 4 * c + 3:4 * c + 4], [gn + "_%d%s" % (k, "d" if e == cut != 32 * b + 32 else side)]
            rd = [sg + "_%d%s" % (h, s) for s in reach] + ["Q4%d" % part]
            if side == "d":
                ts(T.G[:, g0 + 4 * cut + k:g0 + 4 * C:4], T[ps(Q[h])][:, 0:C - cut], T.ST[:, 16 * c:16 * c + 1],
                   T.QS[:, c:c + 1], A.is_le if buyer(t) else A.is_ge, A.mult, [ps(Q[h]), "ST0", "QSd"], wr)
            elif side == "r":
                if e < end:
                    ts(T.G[:, g0 + 4 * e + k:g0 + 4 * end:4], T.SG[:, s0 + 2 * e + h:s0 + 2 * end:2], 0.0, w,
                       A.is_ge, A.mult, rd, wr)
            else:
                out, src = T.G[:, g0 + k:g0 + 4 * e:4], T.SG[:, s0 + h:s0 + 2 * e:2]
                if b not in SCALAR_LEFT:
                    ts(out, src, 0.0, w, A.is_gt, A.mult, rd + [sg + "d"], wr)
                    continue
                if h == 0:
                    cp("s", T.QS[:, c:c + 2], T.Q4[:, 4 * c + 3:4 * c + 8:4], ["Q4%d" % part], ["QS%d" % b])
                act(out, src, AF.Relu, rd + [sg + "d", "QS%d" % b], wr, scale=T.QS[:, c:c + 1])

    def pack(i):
        gq, o, last = "GQ%d" % i, C * i, i == NB // 2 - 1
        rd = [k for side in "lrd" for k in slots("G%d" % i, side)]
        if not last:
            quant("GQ", "GS", o, o + C, T.G[:, 4 * o:4 * (o + C)], rd, parts(gq, UC))
        for k, (a, b) in enumerate(runs(UC)):
            if last:
                quant("GQ", "GS", o + a, o + b, T.G[:, 4 * (o + a):4 * (o + b)], rd, [gq + "_%d" % a])
            mm(P[k], "CQ", "CS", 0, "GQ", "GS", i == 0, last, ["CQ", gq + "_%d" % a], o + a, o + b)

    def early(t):
        first = min(EARLY[t], 2)
        for b, h in [(b, h) for h in range(2) for b in range(first)] + [(b, h) for b in range(first, EARLY[t]) for h in range(2)]:
            sign(t, b, h, "a")
            if (b, h) == (first - 1, 0) and DIRECT[t]:
                n = 2 * max(DIRECT[t]) + 2
                cp("s", T.QS[:, 0:n], T.Q4[:, 3:4 * n:4], ["Q40"], ["QSd"])

    def ahead(t, b):
        ties(t, b)
        weigh(t, b, "r")
        weigh(t, b, "l")

    dma("s", "du", [(T.UB[:], T.u[:], [], ["UB"])])
    for k, (a, b) in enumerate(runs(TC[0])):
        dma("y", "dx%d" % k, [(T.X0[:, 4 * a:4 * b], T.x[:, 4 * a:4 * b], [], slots("X0", k))])
    need("y", ("dx1", 16))
    dma("y", "dw", [(T.WQ[:].bitcast(dt.uint8), T.wc[:], [], ["WQ"]), (T.WS[:], T.ws[:], [], ["WS"])])
    dma("y", "dv", [(T.VB[:], T.v[:], [], ["VB"])])
    iota("PI", T.PI[:], [[15, 2]], 0, 1, True)
    iota("UI", T.UI[:, 0:16], [[16, 2], [32, 4], [0, 2]], 0, 0)
    iota("K16", T.K16[:], [[1, 16]], 0, 0)
    iota("I3", T.I3[:], [[1, 32], [0, 2]], 0, 0)
    iota("I2", T.I2[:], [[1, 8], [0, 32], [-1, 2]], 0, 0)
    fill(T.QP[:], 1000.0, ["QP"])
    fill(T.QP[:, 1:C // 4:4], 1.0, ["QP"])
    ts(T.PJ[:, 0:2], T.PI[:], 15, None, A.bitwise_and, None, ["PI"], ["PJ0"])
    ts(T.PJ[:, 2:3], T.PI[:, 0:1], 31, None, A.bitwise_and, None, ["PI"], ["PJ2"])
    ts(T.PJ[:, 3:4], T.PI[:, 0:1], 4, 6, A.logical_shift_right, A.bitwise_and, ["PI"], ["PJ3"])
    ts(T.PJ[:, 4:5], T.PI[:, 0:1], 2, 3, A.logical_shift_right, A.bitwise_and, ["PI"], ["PJ4"])
    ts(T.PJ[:, 5:6], T.PI[:, 0:1], 8, None, A.bitwise_and, None, ["PI"], ["PJ5"])
    cp("v", T.UO[:, 0:16], T.UI[:, 0:16], ["UI"], ["UO0"])
    cp("v", T.PF[:], T.PJ[:], ["PJ0", "PJ2", "PJ3", "PJ4", "PJ5"], ["PF"])
    ts(T.UO[:, 16:24], T.K16[:, 0:8], 16.0, T.PF[:, 4:5], A.mult, A.add, ["K16", "PF"], ["UO1"])
    ts(T.XA[:], T.K16[:], T.PF[:, 0:1], BIG, A.is_equal, A.mult, ["K16", "PF"], ["XA"])
    ts(T.XB[:], T.K16[:], T.PF[:, 1:2], -2 * BIG, A.is_equal, A.mult, ["K16", "PF"], ["XB"])
    ts(T.RO[:], T.QP[:, 0:K], 0.0, T.PF[:, 0:1], A.mult, A.add, ["QP", "PF"], ["RO"])
    tt(T.XC[:], T.XA[:], T.XB[:], A.add, ["XA", "XB"], ["XC"])
    cp("s", T.XP[:], T.XC[:].indirect(T.RO[:]), ["XC", "RO"], ["XP"])
    quant("UQ", "US", 0, 128, T.UB[:], ["UB"], ["UQ"])
    cp("s", T.UPS[:], T.US[:].indirect(T.UO[:]), ["UQ", "UO0", "UO1"], ["UPS"])
    ts(T.TR[:], T.I3[:], T.PF[:, 2:3], -0.5, A.is_gt, A.mult, ["I3", "PF"], ["TR"])
    cp("v", T.UP[:].bitcast(dt.uint32), T.UQ[:].bitcast(dt.uint32).indirect(T.UO[:]), ["UQ", "UO0", "UO1"], ["UP"])
    act(T.XO[:, 6:7], T.XA[:, 0:1], AF.Identity, ["XA"], ["XO6"], bias=-BIG - 1.0, scale=2.0)
    act(T.XO[:, 0:5], T.K16[:, 0:5], AF.Identity, ["K16", "XO6"], ["XO"], bias=T.XO[:, 6:7], scale=0.5)
    act(T.XO[:, 5:6], T.XC[:, 15:16], AF.Identity, ["XC", "XO"], ["XO5"], bias=T.XO[:, 4:5])
    for j in range(NB // 2):
        for side in "lrd":
            for k in slots("G%d" % j, side):
                writer[k] = []
    state(0, 0)
    for name in ("s0", "e0", "e1"):
        product(0, name)
    state(0, 1)
    turn(0, 0)
    early(0)
    ts(T.CB[:], T.I2[:], T.PF[:, 3:4], None, A.is_equal, None, ["I2", "PF"], ["CB"])
    ts(T.XD[:], T.K16[:], T.PF[:, 5:6], 8.0, A.add, A.is_equal, ["K16", "PF"], ["XD"])
    quant("CQ", "CS", 0, 128, T.CB[:], ["CB"], ["CQ"])
    for b in range(AHEAD[0]):
        ahead(0, b)

    for t in range(2):
        dst = T.cores[rank ^ STEP[t]]
        n = str(t)
        XN, NQ, NS = "X" + str(t + 1), "TQ" + str(t + 1), "TS" + str(t + 1)
        TQ, TS, LQ, LS = "TQ" + n, "TS" + n, "LQ" + n, "LS" + n
        SO, SP, LO, LP, MK, AO = "SO" + n, "SP" + n, "LO" + n, "LP" + n, "MK" + n, "AO" + n
        whole = parts(TQ, TC[t])
        mine, theirs = P[2:] + Q[:2], Q[2:] + P[:2]
        for name in SECOND:
            product(t, name)
        send(dst, "rT" + n, [(T[LQ][:].bitcast(dt.uint8), T[TQ][:].bitcast(dt.uint8), whole, [LQ]),
                             (T[LS][:], T[TS][:], whole, [LS])])
        iota(MK, T[MK][:], [[0, UN]], 0, 0)
        if t == 0:
            iota("ONE", T.ONE[:], [[0, 516]], 1, 0)
            op("g", lambda E: E.affine_select(T.EB[:], T.ONE[:], [[1, 516]], A.is_equal, 0.0, -3, -4), ["ONE"], ["EB"])
            op("g", lambda E: E.affine_select(T.XE[:], T.XP[:], [[0, C]], A.is_equal, 0.0, 0, 0), ["XP"], ["XE"])
            iota("SEG", T.SEG[:, 0:16], [[0, 16]], 0, 0)
            iota("IO", T.IO[:, 0:C], [[1, C]], 0, 0)
        iota(AO, T[AO][:, 0:C], [[0, C]], LOW, 0)
        if t == 0:
            for b in range(4):
                iota("HPz%d" % b, T.HP[:, HW * b + C:HW * b + HW], [[0, HW - C]], 0, 0)
            iota("IOz", T.IO[:, C:HW], [[0, HW - C]], -1, 0)

        def signs(b):
            if b not in DIRECT[t]:
                for h in range(2):
                    sign(t, b, h, "b" if b < EARLY[t] else "ab")

        packed, left = 0, list(range(AHEAD[t]))
        signs(0)
        if AHEAD[t] == 0:
            ties(t, 0)
        for b in range(NB):
            if b in DIRECT[t]:
                weigh(t, b, "d")
            if b + 1 < NB:
                signs(b + 1)
            for c in SCALAR_LEFT:
                if c not in left and c + DELAY <= b:
                    weigh(t, c, "l")
                    left.append(c)
            if AHEAD[t] <= b + 1 < NB:
                ties(t, b + 1)
            if b + 2 == NB:
                for c in SCALAR_LEFT:
                    if c not in left:
                        weigh(t, c, "l")
                        left.append(c)
            if b >= AHEAD[t]:
                weigh(t, b, "r")
            elif b not in DIRECT[t]:
                weigh(t, b, "e")
            if b % 2 == 0 and AHEAD[t] <= b + 1:
                need("v", writer["SG%dd" % (b + 1)][0])
            while packed < b // 2 and 2 * packed in left and 2 * packed + 1 in left:
                pack(packed)
                packed += 1
            if b not in SCALAR_LEFT and b not in left:
                weigh(t, b, "l")
                left.append(b)
            if b == TURN:
                turn(t, 1)
            if t > 0 and b == EARLY[t]:
                unpack(mine, TQ, TS, whole, True, True)
        pack(NB // 2 - 1)
        for k, (a, b) in enumerate(runs(UC)):
            c, d = a // 16, b // 16
            wrap("EX", T[ps(P[k])][:, 0:b - a], [ps(P[k])], ["EX_%d" % a], a, b, "XP")
            ts(T[SO][:, c:d], T.EX[:, a + 15:b:16], T.XO[:, 2:3], None, A.add, None, ["EX_%d" % a, "XO"], [SO + "_%d" % a])
            send(dst, "rS%d%d" % (t, k), [(T[SP][:, c:d], T[SO][:, c:d], [SO + "_%d" % a], [SP + "_%d" % a])])

        def mark(name, a, b):
            cp("v", T[MK][:].indirect(T[name][:, a // 16:b // 16]), T.ONE[:, a:b], parts(name, UC, a, b) + ["ONE"], [MK])

        ts(T.GO[:], T.EX[:, 15:C:16], T.XO[:, 3:4], 0.5, A.add, A.mult, parts("EX", UC) + ["XO"], ["GO"])
        mark(SO, 0, C)
        if t == 0:
            ts(T.XF[:], T.XD[:], -2 * BIG, -AGE, A.mult, A.add, ["XD"], ["XF"])
            for b in range(4):
                quant("EQ", "ES", 128 * b, 128 * b + 128, T.EB[:, 3 - b:515 - b], ["EB"], ["EQ_%d" % b])
            tt(T.XG[:], T.XF[:], T.XA[:], A.add, ["XA", "XF"], ["XG"])
            unpack(mine, TQ, TS, whole, True, True)
        ts(T.EO[:], T.GO[:], -2.0, T.XO[:, 5:6], A.mult, A.add, ["GO", "XO5"], ["EO"])
        tt(T.XE[:, 15:C:16], T.EX[:, 15:C:16], T.EO[:], A.add, parts("EX", UC) + ["EO"], ["XE"])
        mark(SP, *runs(UC)[0])
        unpack(theirs, LQ, LS, [LQ, LS], True, True)
        (a0, cut), (cut, a1) = runs(TC[t + 1])
        for i, bank in enumerate(mine + theirs):
            if i == BEFORE[t]:
                for a, c in runs(UC)[1:]:
                    mark(SP, a, c)
                scan(T.SEG[:, 1:UN // 2 + 1], T[MK][:, 0:UN:2], T[MK][:, 1:UN:2], 0.0, A.add, A.add, [MK], ["SEG"])
                for k in range(2):
                    cp("vs"[k], T.FR[:, C // 2 * k:C // 2 * (k + 1)],
                       T.SEG[:, 0:UN // 2 + 1].indirect(T.GO[:, K // 2 * k:K // 2 * (k + 1)]), ["SEG", "GO"], ["FR%d" % k])
                if t == 0:
                    cp("s", T.XH[:], T.XG[:].indirect(T.RO[:]), ["XG", "RO"], ["XH"])
            name, b = ("DO", "DP")[i // 4], i % 4
            act(T[name][:, C * b:C * b + C], T[ps(bank)][:, 0:C], AF.Copy, [ps(bank)], [name + "_%d" % b], scale=0.5)
            if i < 4:
                cp("s", T.DT[:, C * b + cut:C * b + C], T[ps(bank)][:, cut:C], [ps(bank)], ["DT_%d" % b])
        unpack(P, TQ, TS, whole, True, False, 0, cut)
        wrap("EY", T.FR[:], ["FR0", "FR1"], ["EY"], 0, C, "XE")
        ts(T.FS[:], T.EY[:, 15:C:16], T.XO[:, 0:1], None, A.add, None, ["EY", "XO"], ["FS"])
        cp("v", T[AO][:].indirect(T.FS[:]), T.IO[:, 0:C], ["FS", "IO"], [AO])
        for k, (a, b) in enumerate(runs(LC)):
            c, d, e = a // 16, b // 16, "_%d" % a
            wrap("EZ", T[AO][:, a:b], [AO] + ["EZ_%d" % LC[k - 1]] * (k > 0), ["EZ" + e], a, b, "XH",
                 T.EZ[:, a - 1:a] if k else float(LOW))
            tt(T.LI[:, c:d], T.EZ[:, a + 7:b:16], T.EZ[:, a + 15:b:16], A.max, ["EZ" + e], ["LI" + e])
            ts(T.LJ[:, c:d], T.LI[:, c:d], int(AGE) - 1, None, A.bitwise_and, None, ["LI" + e], ["LJ" + e])
            cp("v", T[LO][:, c:d], T.LJ[:, c:d], ["LJ" + e], [LO + e])
            send(dst, "rL%d%d" % (t, k), [(T[LP][:, c:d], T[LO][:, c:d], [LO + e], [LP + e])])
        ts(T.FO[:], T.EY[:, 15:C:16], T.XO[:, 0:1], float(C), A.add, A.min, ["EY", "XO"], ["FO"])
        for k, (a, b) in enumerate(runs(LC)):
            for i in range(4):
                cp(OWN_ON[k][i], T.ZT[:, C * i + a:C * i + b], T.DO[:, C * i:C * i + C].indirect(T[LO][:, a // 16:b // 16]),
                   ["DO_%d" % i, LO + "_%d" % a], ["ZT%d_%d" % (i, a)])
        if t == 1:
            quant("VQ", "VS", 0, 128, T.VB[:], ["VB"], ["VQ"])
            cp("s", T.OL[:], T.IO[:].indirect(T.FO[:]), ["IO", "IOz", "FO"], ["OL"])
            dma("y", "dol", [(T.ol[:], T.OL[0:128:16, :], ["OL"], [])])

        def pick(k, i):
            a, b = runs(TC[t + 1])[k]
            cp(PICK_ON[k][i], T.HT[:, 4 * a + i:4 * b:4], T.HP[:, HW * i:HW * i + HW].indirect(T.FO[:, a // 16:b // 16]),
               parts("HP%d" % i, ZC) + ["HPz%d" % i, "FO"], ["HT_%d%d" % (i, k)])

        for a, b in runs(ZC):
            for i in range(4):
                tt(T.Z[:, 4 * a + i:4 * b:4], T.DP[:, C * i:C * i + C].indirect(T[LP][:, a // 16:b // 16]),
                   T.ZT[:, C * i + a:C * i + b], A.add, ["DP_%d" % i] + parts(LP, LC, a, b) + parts("ZT%d" % i, LC, a, b),
                   ["Z_%d_%d" % (i, a)])
            quant("ZQ", "ZS", a, b, T.Z[:, 4 * a:4 * b], slots("Z", "_%d" % a), ["ZQ_%d" % a])
            for i in range(4):
                mm(Q[i], "WQ", "WS", 128 * i, "ZQ", "ZS", True, True, ["WQ", "WS", "ZQ_%d" % a], a, b)
            for i in range(4):
                out, src, names = T.HP[:, HW * i + a:HW * i + b], T[ps(Q[i])][:, 0:b - a], ([ps(Q[i])], ["HP%d_%d" % (i, a)])
                if b == C and PICK_ON[0][i] == "v":
                    ts(out, src, 0.0, 0.03125, A.max, A.mult, *names)
                else:
                    act(out, src, AF.Relu, *names, scale=0.03125)
                if b == C:
                    pick(0, i)
        quant("HQ", "HS", 0, cut, T.HT[:, 0:4 * cut], slots("HT", 0), ["HQ_0"])
        unpack(P, "HQ", "HS", ["HQ_0"], False, True, 0, cut)
        for i in range(4):
            pick(1, i)
        quant("HQ", "HS", cut, C, T.HT[:, 4 * cut:4 * C], slots("HT", 1), ["HQ_1"])
        for i in range(4):
            cp("s", T[XN][:, i:4 * cut:4], T[ps(P[i])][:, 0:cut], [ps(P[i])], [XN + "_%d0" % i])
        state(t + 1, 0)
        for name in OPENING:
            i = int(name[1])
            if name[0] == "x":
                unpack(Q, "HQ", "HS", ["HQ_1"], True, True, cut, C, [i])
                tt(T[XN][:, 4 * cut + i:4 * C:4], T[ps(Q[i])][:, 0:C - cut], T.DT[:, C * i + cut:C * i + C], A.add,
                   [ps(Q[i]), "DT_%d" % i], [XN + "_%d1" % i])
            elif t == 0:
                product(1, name)
                if name == "s0":
                    turn(1, 0)
                if name == "e1":
                    early(1)
                    for b in range(FIRST):
                        ahead(1, b)
        state(t + 1, 1)
        if t == 0:
            for b in range(FIRST, AHEAD[1]):
                ahead(1, b)
    for k, (a, b) in enumerate(runs(TC[2])):
        mm((P, Q)[k][0], "VQ", "VS", 0, NQ, NS, True, True, ["VQ", NQ + "_%d" % a], a, b)

    def store(e, out, in_, rd):
        order(e, rd, [], False)
        q[e].dma_start(out, in_).then_inc(T.sem["dst"], 16)
        total["dst"] += 16

    def codes(k):
        a, b = runs(TC[2])[k]
        store("y", T.oc[:, 4 * a:4 * b], T.TQ2[:, a:b].bitcast(dt.uint8), ["TQ2_%d" % a])

    def scales(e, k):
        store(e, T.osc[4 * k:4 * k + 4, :], T.TS2[32 * k:32 * k + 4, :], parts("TQ2", TC[2]))

    def result(k):
        a, b = runs(TC[2])[k]
        bank = ps((P, Q)[k][0])
        cp("sv"[k], T.YS[:, a:b], T[bank][:, 0:b - a], [bank], ["YS%d" % k])
        store("s", T.y[:, a:b], T.YS[:, a:b], ["YS%d" % k])

    codes(0)
    result(0)
    codes(1)
    scales("s", 0)
    result(1)
    scales("y", 1)
    scales("y", 2)
    scales("s", 3)
    for s in SEMAPHORES:
        if total[s] > waited[s]:
            q["y" if s == "dst" else "g"].wait_ge(T.sem[s], total[s])
